import numpy as np
import ml_dtypes


def mxq(x, axis, fmt="e4m3"):
    dtype, down = {"e4m3": (ml_dtypes.float8_e4m3fn, 7), "e5m2": (ml_dtypes.float8_e5m2, 14)}[fmt]
    v = np.moveaxis(np.asarray(x, np.float32).astype(ml_dtypes.bfloat16).astype(np.float64), axis, -1)
    blocks = v.reshape(v.shape[:-1] + (-1, 32))
    amax = np.abs(blocks).max(-1, keepdims=True)
    byte = np.maximum(np.where(amax > 0, np.frexp(amax)[1] - 1 + 127, 0) - down, 1)
    scale = np.exp2(byte - 127.0)
    codes = (blocks / scale).astype(np.float32).astype(dtype).astype(np.float64)
    return np.moveaxis((codes * scale).reshape(v.shape), -1, axis)


WIDE = False


def mx_kscale(k):
    if not WIDE:
        return np.ones(k)
    levels = np.array([10, -10, 5, -5, 0])
    if k % 512:
        return np.exp2(np.random.permutation(np.resize(levels, k // 32))).repeat(32)
    a = np.empty((k // 512, 16))
    for p in range(k // 512):
        a[p, :8] = np.random.permutation(np.resize(levels, 8))
        for g in range(8):
            far = levels[np.abs(levels - a[p, g]) >= 10]
            a[p, g + 8] = far[np.random.randint(len(far))]
    return np.exp2(a.ravel()).repeat(32)


def f64(x):
    return np.asarray(x).astype(np.float64)


def striped(idx):
    return np.tile(np.asarray(idx).reshape(-1, 16).T, (8, 1)).astype(np.uint16)


def unstriped(offs):
    return offs[:16].T.reshape(-1).astype(np.int64)


B, N, T, D, DV, NQ = 1, 1024, 4096, 512, 512, 128


def setup_inputs():
    n = np.random.standard_normal
    idx = np.sort(np.random.permutation(T)[:B * N].reshape(B, N), axis=1).reshape(-1)
    s = mx_kscale(D)[:, None]
    u = np.ones(T)
    u[idx] = mx_kscale(B * N)
    r = np.random.uniform(0.5, 2.0, T)
    raw = n((D, T)) / s / (u * r)
    when = np.zeros(T)
    when[idx] = np.sort(np.random.permutation(2 * N)[:B * N])
    return {
        "qT": (n((B, D, NQ)) * s * (0.80 / np.sqrt(D))).astype(np.float32),
        "cT": raw.astype(np.float32),
        "ts": np.tile(u * r, (128, 1)).astype(np.float32),
        "pos": np.tile(when, (128, 1)).astype(np.float32),
        "slope": np.exp2(-np.random.randint(8, 13, (B, NQ, 1))).astype(np.float32),
        "ch": np.tile(s[:, 0] * np.random.uniform(0.5, 2.0, D), (128, 1)).astype(np.float32),
        "offs": striped(idx),
    }


def reference(qT, cT, ts, pos, slope, ch, offs):
    idx = unstriped(offs)
    c = f64(cT)
    pick = lambda x: x[:, idx].reshape(x.shape[0], B, N).transpose(1, 0, 2)
    q = f64(qT)
    score = mxq(q, 1, "e4m3").transpose(0, 2, 1) @ mxq(pick(c), 1, "e4m3")
    score = score * pick(f64(ts))[:, :1, :]
    score = score + f64(slope) * pick(f64(pos))[:, :1, :]
    m = score.max(-1, keepdims=True)
    p = np.exp(score - m)
    total = p.sum(-1, keepdims=True)
    w = p * pick(f64(ts))[:, :1, :]
    y = mxq(w, 2, "e4m3") @ mxq(pick(c).transpose(0, 2, 1), 1, "e4m3")
    y = y / total
    y = y * f64(ch)[:1]
    return y

@@ -1,0 +1,263 @@
+from contextlib import ExitStack
+
+import concourse.mybir as mybir
+from concourse.masks import make_identity
+
+NQ, N, T, D = 128, 1024, 4096, 512
+P = 128
+PACK = 4
+HALF = 512
+
+F32 = mybir.dt.float32
+BF16 = mybir.dt.bfloat16
+U32 = mybir.dt.uint32
+U16 = mybir.dt.uint16
+U8 = mybir.dt.uint8
+FP8X4 = mybir.dt.float8_e4m3fn_x4
+ACT = mybir.ActivationFunctionType
+ALU = mybir.AluOpType
+AX = mybir.AxisListType
+
+FLOPS = 2 * 2 * NQ * N * D
+BYTES = 4 * (D * T + D * NQ + 2 * T + NQ + D + NQ * D) + 2 * P * N // 16
+
+
+def tile_attend_x_mla_alibi_srt_kernel(tc, qT, cT, ts, pos, slope, ch, offs, out):
+    nc = tc.nc
+    with ExitStack() as ctx:
+        keep = ctx.enter_context(tc.tile_pool(name="keep", bufs=1))
+        psum2 = ctx.enter_context(tc.psum_pool(name="psum2", bufs=2))
+        psum1 = ctx.enter_context(tc.psum_pool(name="psum1", bufs=1))
+
+        offsets = keep.tile([P, N // 16], U16, name="offsets")
+        nc.sync.dma_start(offsets[:], offs)
+
+        planes = []
+        for t in range(PACK):
+            plane = keep.tile([P, T], F32, name=f"plane{t}")
+            planes.append(plane)
+        tsw = keep.tile([P, T], F32, name="tsw")
+        posw = keep.tile([P, T], F32, name="posw")
+        slope_col = keep.tile([NQ, 1], F32, name="slope_col")
+        slope_row = keep.tile([P, NQ], F32, name="slope_row")
+        q_raw = keep.tile([P, PACK, NQ], F32, name="q_raw")
+        ch_sb = keep.tile([P, D], F32, name="ch_sb")
+
+        c_view = cT.rearrange("(p t) n -> t p n", t=PACK)
+        nc.sync.dma_start(out=planes[0][:], in_=c_view[0])
+        ident_f = keep.tile([P, P], F32, name="ident_f")
+        make_identity(nc, ident_f[:])
+        nc.scalar.dma_start(out=slope_col[:], in_=slope[0])
+        nc.vector.memset(tsw[:], 0.0)
+        nc.vector.memset(planes[1][:, 0:8], 0.0)
+        nc.sync.dma_start(out=tsw[0:1, :], in_=ts[0:1, :])
+        nc.sync.dma_start(out=planes[1][:], in_=c_view[1])
+        nc.vector.memset(posw[:], 0.0)
+        for late in (planes[2], planes[3], ch_sb):
+            nc.vector.memset(late[:, 0:8], 0.0)
+        nc.vector.memset(q_raw[:, 0, 0:8], 0.0)
+        nc.sync.dma_start(out=posw[64:65, :], in_=pos[0:1, :])
+        nc.sync.dma_start(out=planes[2][:], in_=c_view[2])
+        nc.sync.dma_start(out=planes[3][:], in_=c_view[3])
+        nc.sync.dma_start(out=q_raw[:], in_=qT[0].rearrange("(p t) q -> p t q", t=PACK))
+        nc.sync.dma_start(out=ch_sb[:], in_=ch)
+
+        warm = keep.tile([P, 1], F32, name="warm")
+        nc.gpsimd.memset(warm[:], 0.0)
+        nc.scalar.activation(warm[:], warm[:], ACT.Exp)
+
+        def pick(window, label):
+            picked = keep.tile([P, N], F32, name=f"{label}_picked")
+            nc.vector.tensor_copy(picked[:], window[:].indirect(offsets[:]))
+            return picked
+
+        def columns(picked, row, label, strided):
+            cols = keep.tile([P, 2, PACK], F32, name=f"{label}_cols")
+            for h in range(2):
+                turned = psum1.tile([P, PACK, P], F32, name=f"raw{h}" if strided else f"scores{h}")
+                for j in range(PACK):
+                    if strided:
+                        block = picked[:, HALF * h + j : HALF * (h + 1) : PACK]
+                    else:
+                        block = picked[:, HALF * h + P * j : HALF * h + P * (j + 1)]
+                    nc.tensor.transpose(turned[:, j, :], block, ident_f[:])
+                nc.scalar.copy(cols[:, h, :], turned[:, :, row])
+            return cols
+
+        gathered = keep.tile([P, PACK, N], F32, name="gathered")
+        latents = keep.tile([P, N, PACK], BF16, name="latents", align_bytes=64)
+        val_codes = keep.tile([P, 2, 2, PACK, P // 2], U32, name="val_codes", align_bytes=64)
+        val_scales = keep.tile([P, 2, 2, PACK, P // 2], U8, name="val_scales", align_bytes=64)
+        values = []
+        for pair in range(2):
+            grouped = keep.tile([P, 2, 2, 2, P // 2, PACK], BF16, name=f"values{pair}", align_bytes=64)
+            values.append(grouped)
+
+        def turn_values(t):
+            for h in range(2):
+                turned = psum2.tile([P, PACK, P], F32, name="turn")
+                for j in range(PACK):
+                    nc.tensor.transpose(turned[:, j, :], gathered[:, t, HALF * h + j : HALF * (h + 1) : PACK], ident_f[:])
+                nc.scalar.copy(values[t // 2][:, h, :, t % 2], turned[:].rearrange("s j (v e) -> s v e j", v=2))
+
+        def quantize_values(pair):
+            for h in range(2):
+                for v in range(2):
+                    nc.vector.quantize_mx(
+                        out=val_codes[:, h, v, 2 * pair : 2 * pair + 2, :].rearrange("s t e -> s (t e)").bitcast(FP8X4),
+                        scales=val_scales[:, h, v, 2 * pair : 2 * pair + 2, :].rearrange("s t e -> s (t e)"),
+                        in_=values[pair][:, h, v].rearrange("s t e j -> s (t e j)"),
+                    )
+
+        def interleave(copy, first, h):
+            cols = slice(HALF * h, HALF * (h + 1))
+            copy(latents[:, cols, first : first + 2], gathered[:, first : first + 2, cols].rearrange("p t i -> p i t"))
+
+        slope_turned = psum1.tile([P, PACK, NQ], F32, name="scores0")
+        nc.tensor.transpose(slope_turned[:, 0, :], slope_col[:].to_broadcast([NQ, P]), ident_f[:])
+        nc.scalar.copy(slope_row[:], slope_turned[:, 0, :])
+
+        ts_picked = pick(tsw, "ts")
+        nc.vector.tensor_copy(gathered[:, 0, :], planes[0][:].indirect(offsets[:]))
+        ts_cols = columns(ts_picked, 0, "ts", False)
+        ts_spread = columns(ts_picked, 0, "ts_spread", True)
+        turn_values(0)
+        pos_picked = pick(posw, "pos")
+        nc.vector.tensor_copy(gathered[:, 1, :], planes[1][:].indirect(offsets[:]))
+        pos_cols = columns(pos_picked, 64, "pos", False)
+        turn_values(1)
+        bias = keep.tile([P, 2, PACK, NQ], F32, name="bias")
+        for h in range(2):
+            for j in range(PACK):
+                nc.scalar.activation(bias[:, h, j, :], slope_row[:], ACT.Copy, scale=pos_cols[:, h, j : j + 1])
+        interleave(nc.vector.tensor_copy, 0, 0)
+        interleave(nc.vector.tensor_copy, 0, 1)
+        nc.vector.tensor_copy(gathered[:, 2, :], planes[2][:].indirect(offsets[:]))
+        turn_values(2)
+        quantize_values(0)
+
+        key_codes = keep.tile([P, 2, HALF], U32, name="key_codes", align_bytes=64)
+        key_scales = keep.tile([P, 2, HALF], U8, name="key_scales", align_bytes=64)
+        q_grouped = keep.tile([P, NQ, PACK], BF16, name="q_grouped", align_bytes=64)
+        q_codes = keep.tile([P, NQ], U32, name="q_codes", align_bytes=64)
+        q_scales = keep.tile([P, NQ], U8, name="q_scales", align_bytes=64)
+
+        for h in range(2):
+            nc.vector.tensor_copy(
+                gathered[:, 3, HALF * h : HALF * (h + 1)], planes[3][:].indirect(offsets[:, 32 * h : 32 * (h + 1)])
+            )
+        nc.scalar.copy(q_grouped[:], q_raw[:].rearrange("p t q -> p q t"))
+        interleave(nc.scalar.copy, 2, 0)
+        interleave(nc.vector.tensor_copy, 2, 1)
+        nc.vector.quantize_mx(
+            out=q_codes[:].bitcast(FP8X4), scales=q_scales[:], in_=q_grouped[:].rearrange("p q t -> p (q t)")
+        )
+
+        biased = keep.tile([P, 2, PACK, NQ], F32, name="biased")
+        raws = []
+        banks = []
+        for h in range(2):
+            nc.vector.quantize_mx(
+                out=key_codes[:, h, :].bitcast(FP8X4),
+                scales=key_scales[:, h, :],
+                in_=latents[:, HALF * h : HALF * (h + 1), :].rearrange("p i t -> p (i t)"),
+            )
+            raw = psum1.tile([P, PACK, NQ], F32, name=f"raw{h}")
+            for j in range(PACK):
+                block = slice(P * j, P * (j + 1))
+                nc.tensor.matmul_mx(
+                    out=raw[:, j, :],
+                    lhsT=key_codes[:, h, block].bitcast(FP8X4),
+                    lhsT_scale=key_scales[:, h, block],
+                    rhs=q_codes[:].bitcast(FP8X4),
+                    rhs_scale=q_scales[:],
+                    start=True,
+                    stop=True,
+                )
+            raws.append(raw)
+
+        for h in range(2):
+            bank = psum1.tile([NQ, PACK, P], F32, name=f"scores{h}")
+            for j in range(PACK):
+                nc.vector.scalar_tensor_tensor(
+                    biased[:, h, j, :], raws[h][:, j, :], ts_cols[:, h, j : j + 1], bias[:, h, j, :], ALU.mult, ALU.add
+                )
+                nc.tensor.transpose(bank[:, j, :], biased[:, h, j, :], ident_f[:])
+            banks.append(bank)
+
+        negated = keep.tile([NQ, PACK, P], F32, name="negated")
+        floors = keep.tile([NQ, 2], F32, name="floors")
+        nc.vector.tensor_scalar(
+            negated[:], banks[0][:], -1.0, None, ALU.mult, ALU.min, accum_out=floors[:, 0:1]
+        )
+        nc.vector.tensor_scalar(
+            negated[:], banks[1][:], -1.0, floors[:, 0:1], ALU.mult, ALU.min, accum_out=floors[:, 1:2]
+        )
+
+        turn_values(3)
+        quantize_values(1)
+
+        probs = keep.tile([NQ, 2, PACK, P], F32, name="probs")
+        sums = keep.tile([NQ, 3], F32, name="sums")
+        for n, (h, j0, j1) in enumerate(((0, 0, 4), (1, 0, 2), (1, 2, 4))):
+            nc.scalar.activation(
+                probs[:, h, j0:j1],
+                banks[h][:].rearrange("q b m -> q (b m)").rearrange("q (i j) -> q j i", j=PACK)[:, j0:j1],
+                ACT.Exp,
+                bias=floors[:, 1:2],
+                accum_out=sums[:, n : n + 1],
+            )
+        w_codes = keep.tile([P, 2, NQ], U32, name="w_codes", align_bytes=64)
+        w_scales = keep.tile([P, 2, NQ], U8, name="w_scales", align_bytes=64)
+        weights = []
+        for h in range(2):
+            turned = psum2.tile([P, PACK, P], F32, name="turn")
+            for t in range(PACK):
+                nc.tensor.transpose(turned[:, t, :], probs[:, h, t, :], ident_f[:])
+            w = keep.tile([P, NQ, PACK], BF16, name=f"w{h}", align_bytes=64)
+            nc.vector.tensor_tensor(
+                w[:],
+                turned[:].rearrange("s t q -> s q t"),
+                ts_spread[:, h, :].unsqueeze(1).to_broadcast([P, NQ, PACK]),
+                ALU.mult,
+            )
+            weights.append(w)
+        for h in range(2):
+            nc.vector.quantize_mx(
+                out=w_codes[:, h, :].bitcast(FP8X4), scales=w_scales[:, h, :], in_=weights[h][:].rearrange("s q t -> s (q t)")
+            )
+        total = keep.tile([P, 1], F32, name="total")
+        nc.vector.reduce_sum(total[:], sums[:], axis=AX.X)
+        inverse = keep.tile([P, 1], F32, name="inverse")
+        nc.vector.reciprocal(inverse[:], total[:])
+
+        outputs = []
+        for v in range(2):
+            y = psum1.tile([NQ, D // 2], F32, name=f"raw{v}")
+            outputs.append(y)
+        for h in range(2):
+            for v in range(2):
+                nc.tensor.matmul_mx(
+                    out=outputs[v][:],
+                    lhsT=w_codes[:, h, :].bitcast(FP8X4),
+                    lhsT_scale=w_scales[:, h, :],
+                    rhs=val_codes[:, h, v].rearrange("s t e -> s (t e)").bitcast(FP8X4),
+                    rhs_scale=val_scales[:, h, v].rearrange("s t e -> s (t e)"),
+                    start=(h == 0),
+                    stop=(h == 1),
+                )
+        result = keep.tile([NQ, P, PACK], F32, name="result")
+        ch_view = ch_sb[:].rearrange("q (e t) -> q e t", t=PACK)
+        for v, queue in enumerate((nc.scalar, nc.sync)):
+            part = slice(P // 2 * v, P // 2 * (v + 1))
+            nc.vector.scalar_tensor_tensor(
+                result[:, part],
+                outputs[v][:].rearrange("q (t e) -> q e t", t=PACK),
+                inverse[:],
+                ch_view[:, part],
+                ALU.mult,
+                ALU.mult,
+            )
+            queue.dma_start(
+                out=out[0][:, D // 2 * v : D // 2 * (v + 1)], in_=result[:, part].rearrange("q e t -> q (e t)")
+            )

@@ -7,6 +7,7 @@ NQ, N, T, D = 128, 1024, 4096, 512
 P = 128
 PACK = 4
 HALF = 512
+PREFIX = T - HALF
 
 F32 = mybir.dt.float32
 BF16 = mybir.dt.bfloat16
@@ -16,10 +17,12 @@ U8 = mybir.dt.uint8
 FP8X4 = mybir.dt.float8_e4m3fn_x4
 ACT = mybir.ActivationFunctionType
 ALU = mybir.AluOpType
-AX = mybir.AxisListType
 
 FLOPS = 2 * 2 * NQ * N * D
 BYTES = 4 * (D * T + D * NQ + 2 * T + NQ + D + NQ * D) + 2 * P * N // 16
+
+TS_ROW = 127
+POS_ROW = 63
 
 
 def tile_attend_x_mla_alibi_srt_kernel(tc, qT, cT, ts, pos, slope, ch, offs, out):
@@ -32,10 +35,7 @@ def tile_attend_x_mla_alibi_srt_kernel(tc, qT, cT, ts, pos, slope, ch, offs, out
         offsets = keep.tile([P, N // 16], U16, name="offsets")
         nc.sync.dma_start(offsets[:], offs)
 
-        planes = []
-        for t in range(PACK):
-            plane = keep.tile([P, T], F32, name=f"plane{t}")
-            planes.append(plane)
+        planes = [keep.tile([P, T], F32, name=f"plane{t}") for t in range(PACK)]
         tsw = keep.tile([P, T], F32, name="tsw")
         posw = keep.tile([P, T], F32, name="posw")
         slope_col = keep.tile([NQ, 1], F32, name="slope_col")
@@ -44,24 +44,18 @@ def tile_attend_x_mla_alibi_srt_kernel(tc, qT, cT, ts, pos, slope, ch, offs, out
         ch_sb = keep.tile([P, D], F32, name="ch_sb")
 
         c_view = cT.rearrange("(p t) n -> t p n", t=PACK)
-        nc.sync.dma_start(out=planes[0][:], in_=c_view[0])
-        ident_f = keep.tile([P, P], F32, name="ident_f")
-        make_identity(nc, ident_f[:])
+        nc.sync.dma_start(out=tsw[TS_ROW : TS_ROW + 1, :], in_=ts[0:1, :])
+        nc.sync.dma_start(out=posw[POS_ROW : POS_ROW + 1, :], in_=pos[0:1, :])
         nc.scalar.dma_start(out=slope_col[:], in_=slope[0])
-        nc.vector.memset(tsw[:], 0.0)
-        nc.vector.memset(planes[1][:, 0:8], 0.0)
-        nc.sync.dma_start(out=tsw[0:1, :], in_=ts[0:1, :])
-        nc.sync.dma_start(out=planes[1][:], in_=c_view[1])
-        nc.vector.memset(posw[:], 0.0)
-        for late in (planes[2], planes[3], ch_sb):
-            nc.vector.memset(late[:, 0:8], 0.0)
-        nc.vector.memset(q_raw[:, 0, 0:8], 0.0)
-        nc.sync.dma_start(out=posw[64:65, :], in_=pos[0:1, :])
-        nc.sync.dma_start(out=planes[2][:], in_=c_view[2])
-        nc.sync.dma_start(out=planes[3][:], in_=c_view[3])
+        for t in range(PACK - 1):
+            nc.sync.dma_start(out=planes[t][:], in_=c_view[t])
+        nc.sync.dma_start(out=planes[3][:, :PREFIX], in_=c_view[3][:, :PREFIX])
         nc.sync.dma_start(out=q_raw[:], in_=qT[0].rearrange("(p t) q -> p t q", t=PACK))
+        nc.sync.dma_start(out=planes[3][:, PREFIX:], in_=c_view[3][:, PREFIX:])
         nc.sync.dma_start(out=ch_sb[:], in_=ch)
 
+        ident = keep.tile([P, P], F32, name="ident")
+        make_identity(nc, ident[:])
         warm = keep.tile([P, 1], F32, name="warm")
         nc.gpsimd.memset(warm[:], 0.0)
         nc.scalar.activation(warm[:], warm[:], ACT.Exp)
@@ -71,104 +65,104 @@ def tile_attend_x_mla_alibi_srt_kernel(tc, qT, cT, ts, pos, slope, ch, offs, out
             nc.vector.tensor_copy(picked[:], window[:].indirect(offsets[:]))
             return picked
 
-        def columns(picked, row, label, strided):
+        def columns(picked, row, label, bank_name):
             cols = keep.tile([P, 2, PACK], F32, name=f"{label}_cols")
             for h in range(2):
-                turned = psum1.tile([P, PACK, P], F32, name=f"raw{h}" if strided else f"scores{h}")
+                turned = psum1.tile([P, PACK, P], F32, name=f"{bank_name}{h}")
                 for j in range(PACK):
-                    if strided:
-                        block = picked[:, HALF * h + j : HALF * (h + 1) : PACK]
-                    else:
-                        block = picked[:, HALF * h + P * j : HALF * h + P * (j + 1)]
-                    nc.tensor.transpose(turned[:, j, :], block, ident_f[:])
+                    nc.tensor.transpose(turned[:, j, :], picked[:, HALF * h + j : HALF * (h + 1) : PACK], ident[:])
                 nc.scalar.copy(cols[:, h, :], turned[:, :, row])
             return cols
 
-        gathered = keep.tile([P, PACK, N], F32, name="gathered")
-        latents = keep.tile([P, N, PACK], BF16, name="latents", align_bytes=64)
-        val_codes = keep.tile([P, 2, 2, PACK, P // 2], U32, name="val_codes", align_bytes=64)
-        val_scales = keep.tile([P, 2, 2, PACK, P // 2], U8, name="val_scales", align_bytes=64)
-        values = []
-        for pair in range(2):
-            grouped = keep.tile([P, 2, 2, 2, P // 2, PACK], BF16, name=f"values{pair}", align_bytes=64)
-            values.append(grouped)
+        nc.vector.memset(tsw[:TS_ROW, :], 0.0)
+        ts_picked = pick(tsw, "ts")
+        nc.vector.memset(posw[:POS_ROW, :], 0.0)
+        nc.gpsimd.memset(posw[POS_ROW + 1 :, :], 0.0)
+
+        slope_turned = psum1.tile([P, PACK, NQ], F32, name="side0")
+        nc.tensor.transpose(slope_turned[:, 0, :], slope_col[:].to_broadcast([NQ, P]), ident[:])
+        nc.scalar.copy(slope_row[:], slope_turned[:, 0, :])
+        ts_cols = columns(ts_picked, TS_ROW, "ts", "raw")
+
+        low = keep.tile([P, 2, 2, 2, P, 2], BF16, name="low")
+        high = [keep.tile([P, 2, 2, P, 2], BF16, name=f"high{h}") for h in range(2)]
+        latents = [keep.tile([P, 2, 2, P, PACK], BF16, name=f"latents{h}", align_bytes=64) for h in range(2)]
+        values = keep.tile([P, 2, 2, PACK, P // 2, 2], F32, name="values", align_bytes=64)
+
+        def picked_pair(t, h):
+            return low[:, :, :, h] if t < 2 else high[h][:]
+
+        def gather_low(t):
+            nc.vector.tensor_copy(low[:, t].rearrange("p u h s e -> p (h s) u e"), planes[t][:].indirect(offsets[:]))
+
+        def gather_high(t, h):
+            width = PREFIX if h == 0 else T
+            nc.vector.tensor_copy(
+                high[h][:, t - 2].rearrange("p u s e -> p s u e"),
+                planes[t][:, :width].indirect(offsets[:, 32 * h : 32 * (h + 1)]),
+            )
 
         def turn_values(t):
+            turned = psum2.tile([P, 2, 2, P], F32, name="turn")
             for h in range(2):
-                turned = psum2.tile([P, PACK, P], F32, name="turn")
-                for j in range(PACK):
-                    nc.tensor.transpose(turned[:, j, :], gathered[:, t, HALF * h + j : HALF * (h + 1) : PACK], ident_f[:])
-                nc.scalar.copy(values[t // 2][:, h, :, t % 2], turned[:].rearrange("s j (v e) -> s v e j", v=2))
-
-        def quantize_values(pair):
-            for h in range(2):
-                for v in range(2):
-                    nc.vector.quantize_mx(
-                        out=val_codes[:, h, v, 2 * pair : 2 * pair + 2, :].rearrange("s t e -> s (t e)").bitcast(FP8X4),
-                        scales=val_scales[:, h, v, 2 * pair : 2 * pair + 2, :].rearrange("s t e -> s (t e)"),
-                        in_=values[pair][:, h, v].rearrange("s t e j -> s (t e j)"),
-                    )
+                for u in range(2):
+                    words = picked_pair(t, h)[:, t % 2, u].rearrange("p s e -> p (s e)").bitcast(F32)
+                    nc.tensor.transpose(turned[:, h, u, :], words, ident[:])
+            nc.scalar.copy(values[:, :, :, t], turned[:].rearrange("s h u (v c) -> s h v c u", v=2))
 
         def interleave(copy, first, h):
-            cols = slice(HALF * h, HALF * (h + 1))
-            copy(latents[:, cols, first : first + 2], gathered[:, first : first + 2, cols].rearrange("p t i -> p i t"))
+            copy(latents[h][:, :, :, :, first : first + 2], picked_pair(first, h).rearrange("p t u s e -> p u e s t"))
 
-        slope_turned = psum1.tile([P, PACK, NQ], F32, name="scores0")
-        nc.tensor.transpose(slope_turned[:, 0, :], slope_col[:].to_broadcast([NQ, P]), ident_f[:])
-        nc.scalar.copy(slope_row[:], slope_turned[:, 0, :])
-
-        ts_picked = pick(tsw, "ts")
-        nc.vector.tensor_copy(gathered[:, 0, :], planes[0][:].indirect(offsets[:]))
-        ts_cols = columns(ts_picked, 0, "ts", False)
-        ts_spread = columns(ts_picked, 0, "ts_spread", True)
-        turn_values(0)
+        gather_low(0)
         pos_picked = pick(posw, "pos")
-        nc.vector.tensor_copy(gathered[:, 1, :], planes[1][:].indirect(offsets[:]))
-        pos_cols = columns(pos_picked, 64, "pos", False)
-        turn_values(1)
+        turn_values(0)
+        pos_cols = columns(pos_picked, POS_ROW, "pos", "side")
         bias = keep.tile([P, 2, PACK, NQ], F32, name="bias")
+        banks = []
         for h in range(2):
+            bank = psum1.tile([NQ, PACK, P], F32, name=f"scores{h}")
             for j in range(PACK):
                 nc.scalar.activation(bias[:, h, j, :], slope_row[:], ACT.Copy, scale=pos_cols[:, h, j : j + 1])
-        interleave(nc.vector.tensor_copy, 0, 0)
-        interleave(nc.vector.tensor_copy, 0, 1)
-        nc.vector.tensor_copy(gathered[:, 2, :], planes[2][:].indirect(offsets[:]))
+                nc.tensor.matmul(bank[:, j, :], bias[:, h, j, :], ident[:], start=(j == 0), stop=False, is_transpose=True)
+            banks.append(bank)
+        gather_low(1)
+        turn_values(1)
+        for h in range(2):
+            interleave(nc.scalar.copy, 0, h)
+        for h in range(2):
+            gather_high(2, h)
         turn_values(2)
-        quantize_values(0)
 
-        key_codes = keep.tile([P, 2, HALF], U32, name="key_codes", align_bytes=64)
-        key_scales = keep.tile([P, 2, HALF], U8, name="key_scales", align_bytes=64)
+        key_codes = [keep.tile([P, HALF], U32, name=f"key_codes{h}", align_bytes=64) for h in range(2)]
+        key_scales = [keep.tile([P, HALF], U8, name=f"key_scales{h}", align_bytes=64) for h in range(2)]
         q_grouped = keep.tile([P, NQ, PACK], BF16, name="q_grouped", align_bytes=64)
         q_codes = keep.tile([P, NQ], U32, name="q_codes", align_bytes=64)
         q_scales = keep.tile([P, NQ], U8, name="q_scales", align_bytes=64)
 
         for h in range(2):
-            nc.vector.tensor_copy(
-                gathered[:, 3, HALF * h : HALF * (h + 1)], planes[3][:].indirect(offsets[:, 32 * h : 32 * (h + 1)])
-            )
+            gather_high(3, h)
         nc.scalar.copy(q_grouped[:], q_raw[:].rearrange("p t q -> p q t"))
         interleave(nc.scalar.copy, 2, 0)
-        interleave(nc.vector.tensor_copy, 2, 1)
         nc.vector.quantize_mx(
             out=q_codes[:].bitcast(FP8X4), scales=q_scales[:], in_=q_grouped[:].rearrange("p q t -> p (q t)")
         )
+        interleave(nc.vector.tensor_copy, 2, 1)
+        turn_values(3)
 
-        biased = keep.tile([P, 2, PACK, NQ], F32, name="biased")
         raws = []
-        banks = []
         for h in range(2):
             nc.vector.quantize_mx(
-                out=key_codes[:, h, :].bitcast(FP8X4),
-                scales=key_scales[:, h, :],
-                in_=latents[:, HALF * h : HALF * (h + 1), :].rearrange("p i t -> p (i t)"),
+                out=key_codes[h][:].bitcast(FP8X4),
+                scales=key_scales[h][:],
+                in_=latents[h][:].rearrange("p u e s t -> p (u e s t)"),
             )
             raw = psum1.tile([P, PACK, NQ], F32, name=f"raw{h}")
             for j in range(PACK):
                 block = slice(P * j, P * (j + 1))
                 nc.tensor.matmul_mx(
                     out=raw[:, j, :],
-                    lhsT=key_codes[:, h, block].bitcast(FP8X4),
-                    lhsT_scale=key_scales[:, h, block],
+                    lhsT=key_codes[h][:, block].bitcast(FP8X4),
+                    lhsT_scale=key_scales[h][:, block],
                     rhs=q_codes[:].bitcast(FP8X4),
                     rhs_scale=q_scales[:],
                     start=True,
@@ -176,73 +170,81 @@ def tile_attend_x_mla_alibi_srt_kernel(tc, qT, cT, ts, pos, slope, ch, offs, out
                 )
             raws.append(raw)
 
-        for h in range(2):
-            bank = psum1.tile([NQ, PACK, P], F32, name=f"scores{h}")
-            for j in range(PACK):
-                nc.vector.scalar_tensor_tensor(
-                    biased[:, h, j, :], raws[h][:, j, :], ts_cols[:, h, j : j + 1], bias[:, h, j, :], ALU.mult, ALU.add
-                )
-                nc.tensor.transpose(bank[:, j, :], biased[:, h, j, :], ident_f[:])
-            banks.append(bank)
-
-        negated = keep.tile([NQ, PACK, P], F32, name="negated")
-        floors = keep.tile([NQ, 2], F32, name="floors")
-        nc.vector.tensor_scalar(
-            negated[:], banks[0][:], -1.0, None, ALU.mult, ALU.min, accum_out=floors[:, 0:1]
+        scaled = [keep.tile([P, PACK, NQ], F32, name=f"scaled{h}") for h in range(2)]
+        for j in range(PACK):
+            nc.scalar.activation(scaled[0][:, j, :], raws[0][:, j, :], ACT.Copy, scale=ts_cols[:, 0, j : j + 1])
+        nc.vector.tensor_tensor(
+            scaled[1][:], raws[1][:], ts_cols[:, 1, :].unsqueeze(2).to_broadcast([P, PACK, NQ]), ALU.mult
         )
+        for h in range(2):
+            for j in range(PACK):
+                nc.tensor.matmul(
+                    banks[h][:, j, :], scaled[h][:, j, :], ident[:], start=False, stop=(j == PACK - 1), is_transpose=True
+                )
+
+        negated = keep.tile([NQ, PACK, P], F32, name="val_codes", align_bytes=64)
+        floors = keep.tile([NQ, 2], F32, name="floors")
+        nc.vector.tensor_scalar(negated[:], banks[0][:], -1.0, None, ALU.mult, ALU.min, accum_out=floors[:, 0:1])
         nc.vector.tensor_scalar(
             negated[:], banks[1][:], -1.0, floors[:, 0:1], ALU.mult, ALU.min, accum_out=floors[:, 1:2]
         )
 
-        turn_values(3)
-        quantize_values(1)
+        val_codes = keep.tile([P, 2, D], U32, name="val_codes", align_bytes=64)
+        val_scales = keep.tile([P, 2, D], U8, name="val_scales", align_bytes=64)
+        for h in range(2):
+            nc.vector.quantize_mx(
+                out=val_codes[:, h, :].bitcast(FP8X4),
+                scales=val_scales[:, h, :],
+                in_=values[:, h].rearrange("s v t c u -> s (v t c u)").bitcast(BF16),
+            )
 
         probs = keep.tile([NQ, 2, PACK, P], F32, name="probs")
-        sums = keep.tile([NQ, 3], F32, name="sums")
-        for n, (h, j0, j1) in enumerate(((0, 0, 4), (1, 0, 2), (1, 2, 4))):
-            nc.scalar.activation(
-                probs[:, h, j0:j1],
-                banks[h][:].rearrange("q b m -> q (b m)").rearrange("q (i j) -> q j i", j=PACK)[:, j0:j1],
-                ACT.Exp,
-                bias=floors[:, 1:2],
-                accum_out=sums[:, n : n + 1],
-            )
+        sums = keep.tile([NQ, 4], F32, name="sums")
+        for h in range(2):
+            for u in range(2):
+                nc.scalar.activation(
+                    probs[:, h, 2 * u : 2 * u + 2],
+                    banks[h][:, 2 * u : 2 * u + 2],
+                    ACT.Exp,
+                    bias=floors[:, 1:2],
+                    accum_out=sums[:, 2 * h + u : 2 * h + u + 1],
+                )
+        sums_copy = keep.tile([NQ, 4], F32, name="sums_copy")
+        total = keep.tile([NQ, 1], F32, name="total")
+        nc.scalar.activation(sums_copy[:], sums[:], ACT.Copy, accum_out=total[:])
+
         w_codes = keep.tile([P, 2, NQ], U32, name="w_codes", align_bytes=64)
         w_scales = keep.tile([P, 2, NQ], U8, name="w_scales", align_bytes=64)
         weights = []
         for h in range(2):
-            turned = psum2.tile([P, PACK, P], F32, name="turn")
-            for t in range(PACK):
-                nc.tensor.transpose(turned[:, t, :], probs[:, h, t, :], ident_f[:])
+            turned = psum1.tile([P, PACK, NQ], F32, name=f"side{h}")
+            for j in range(PACK):
+                nc.tensor.transpose(turned[:, j, :], probs[:, h, j, :], ident[:])
             w = keep.tile([P, NQ, PACK], BF16, name=f"w{h}", align_bytes=64)
             nc.vector.tensor_tensor(
                 w[:],
-                turned[:].rearrange("s t q -> s q t"),
-                ts_spread[:, h, :].unsqueeze(1).to_broadcast([P, NQ, PACK]),
+                turned[:].rearrange("s j q -> s q j"),
+                ts_cols[:, h, :].unsqueeze(1).to_broadcast([P, NQ, PACK]),
                 ALU.mult,
             )
             weights.append(w)
         for h in range(2):
             nc.vector.quantize_mx(
-                out=w_codes[:, h, :].bitcast(FP8X4), scales=w_scales[:, h, :], in_=weights[h][:].rearrange("s q t -> s (q t)")
+                out=w_codes[:, h, :].bitcast(FP8X4), scales=w_scales[:, h, :], in_=weights[h][:].rearrange("s q j -> s (q j)")
             )
-        total = keep.tile([P, 1], F32, name="total")
-        nc.vector.reduce_sum(total[:], sums[:], axis=AX.X)
-        inverse = keep.tile([P, 1], F32, name="inverse")
+        inverse = keep.tile([NQ, 1], F32, name="inverse")
         nc.vector.reciprocal(inverse[:], total[:])
 
-        outputs = []
-        for v in range(2):
-            y = psum1.tile([NQ, D // 2], F32, name=f"raw{v}")
-            outputs.append(y)
+        outputs = [psum1.tile([NQ, D // 2], F32, name=f"raw{v}") for v in range(2)]
         for h in range(2):
             for v in range(2):
+                cols = slice(D // 2 * v, D // 2 * (v + 1))
                 nc.tensor.matmul_mx(
                     out=outputs[v][:],
                     lhsT=w_codes[:, h, :].bitcast(FP8X4),
                     lhsT_scale=w_scales[:, h, :],
-                    rhs=val_codes[:, h, v].rearrange("s t e -> s (t e)").bitcast(FP8X4),
-                    rhs_scale=val_scales[:, h, v].rearrange("s t e -> s (t e)"),
+                    rhs=val_codes[:, h, cols].bitcast(FP8X4),
+                    rhs_scale=val_scales[:, h, cols],
                     start=(h == 0),
                     stop=(h == 1),
                 )

@@ -74,15 +74,15 @@ def tile_attend_x_mla_alibi_srt_kernel(tc, qT, cT, ts, pos, slope, ch, offs, out
                 nc.scalar.copy(cols[:, h, :], turned[:, :, row])
             return cols
 
+        nc.vector.memset(posw[:POS_ROW, :], 0.0)
+        nc.vector.memset(posw[POS_ROW + 1 :, :], 0.0)
+        pos_picked = pick(posw, "pos")
         nc.vector.memset(tsw[:TS_ROW, :], 0.0)
         ts_picked = pick(tsw, "ts")
-        nc.vector.memset(posw[:POS_ROW, :], 0.0)
-        nc.gpsimd.memset(posw[POS_ROW + 1 :, :], 0.0)
 
         slope_turned = psum1.tile([P, PACK, NQ], F32, name="side0")
         nc.tensor.transpose(slope_turned[:, 0, :], slope_col[:].to_broadcast([NQ, P]), ident[:])
         nc.scalar.copy(slope_row[:], slope_turned[:, 0, :])
-        ts_cols = columns(ts_picked, TS_ROW, "ts", "raw")
 
         low = keep.tile([P, 2, 2, 2, P, 2], BF16, name="low")
         high = [keep.tile([P, 2, 2, P, 2], BF16, name=f"high{h}") for h in range(2)]
@@ -113,9 +113,6 @@ def tile_attend_x_mla_alibi_srt_kernel(tc, qT, cT, ts, pos, slope, ch, offs, out
         def interleave(copy, first, h):
             copy(latents[h][:, :, :, :, first : first + 2], picked_pair(first, h).rearrange("p t u s e -> p u e s t"))
 
-        gather_low(0)
-        pos_picked = pick(posw, "pos")
-        turn_values(0)
         pos_cols = columns(pos_picked, POS_ROW, "pos", "side")
         bias = keep.tile([P, 2, PACK, NQ], F32, name="bias")
         banks = []
@@ -125,12 +122,15 @@ def tile_attend_x_mla_alibi_srt_kernel(tc, qT, cT, ts, pos, slope, ch, offs, out
                 nc.scalar.activation(bias[:, h, j, :], slope_row[:], ACT.Copy, scale=pos_cols[:, h, j : j + 1])
                 nc.tensor.matmul(bank[:, j, :], bias[:, h, j, :], ident[:], start=(j == 0), stop=False, is_transpose=True)
             banks.append(bank)
+        ts_cols = columns(ts_picked, TS_ROW, "ts", "raw")
+        gather_low(0)
+        turn_values(0)
         gather_low(1)
         turn_values(1)
-        for h in range(2):
-            interleave(nc.scalar.copy, 0, h)
+        interleave(nc.scalar.copy, 0, 0)
         for h in range(2):
             gather_high(2, h)
+        interleave(nc.vector.tensor_copy, 0, 1)
         turn_values(2)
 
         key_codes = [keep.tile([P, HALF], U32, name=f"key_codes{h}", align_bytes=64) for h in range(2)]

@@ -21,8 +21,7 @@ ALU = mybir.AluOpType
 FLOPS = 2 * 2 * NQ * N * D
 BYTES = 4 * (D * T + D * NQ + 2 * T + NQ + D + NQ * D) + 2 * P * N // 16
 
-TS_ROW = 127
-POS_ROW = 63
+ROW = 127
 
 
 def tile_attend_x_mla_alibi_srt_kernel(tc, qT, cT, ts, pos, slope, ch, offs, out):
@@ -44,9 +43,9 @@ def tile_attend_x_mla_alibi_srt_kernel(tc, qT, cT, ts, pos, slope, ch, offs, out
         ch_sb = keep.tile([P, D], F32, name="ch_sb")
 
         c_view = cT.rearrange("(p t) n -> t p n", t=PACK)
-        nc.sync.dma_start(out=tsw[TS_ROW : TS_ROW + 1, :], in_=ts[0:1, :])
-        nc.sync.dma_start(out=posw[POS_ROW : POS_ROW + 1, :], in_=pos[0:1, :])
         nc.scalar.dma_start(out=slope_col[:], in_=slope[0])
+        nc.scalar.dma_start(out=posw[ROW:, :], in_=pos[0:1, :])
+        nc.scalar.dma_start(out=tsw[ROW:, :], in_=ts[0:1, :])
         for t in range(PACK - 1):
             nc.sync.dma_start(out=planes[t][:], in_=c_view[t])
         nc.sync.dma_start(out=planes[3][:, :PREFIX], in_=c_view[3][:, :PREFIX])
@@ -56,9 +55,6 @@ def tile_attend_x_mla_alibi_srt_kernel(tc, qT, cT, ts, pos, slope, ch, offs, out
 
         ident = keep.tile([P, P], F32, name="ident")
         make_identity(nc, ident[:])
-        warm = keep.tile([P, 1], F32, name="warm")
-        nc.gpsimd.memset(warm[:], 0.0)
-        nc.scalar.activation(warm[:], warm[:], ACT.Exp)
 
         def pick(window, label):
             picked = keep.tile([P, N], F32, name=f"{label}_picked")
@@ -74,10 +70,9 @@ def tile_attend_x_mla_alibi_srt_kernel(tc, qT, cT, ts, pos, slope, ch, offs, out
                 nc.scalar.copy(cols[:, h, :], turned[:, :, row])
             return cols
 
-        nc.vector.memset(posw[:POS_ROW, :], 0.0)
-        nc.vector.memset(posw[POS_ROW + 1 :, :], 0.0)
+        nc.vector.memset(posw[:ROW, :], 0.0)
         pos_picked = pick(posw, "pos")
-        nc.vector.memset(tsw[:TS_ROW, :], 0.0)
+        nc.gpsimd.memset(tsw[:ROW, :], 0.0)
         ts_picked = pick(tsw, "ts")
 
         slope_turned = psum1.tile([P, PACK, NQ], F32, name="side0")
@@ -113,7 +108,7 @@ def tile_attend_x_mla_alibi_srt_kernel(tc, qT, cT, ts, pos, slope, ch, offs, out
         def interleave(copy, first, h):
             copy(latents[h][:, :, :, :, first : first + 2], picked_pair(first, h).rearrange("p t u s e -> p u e s t"))
 
-        pos_cols = columns(pos_picked, POS_ROW, "pos", "side")
+        pos_cols = columns(pos_picked, ROW, "pos", "side")
         bias = keep.tile([P, 2, PACK, NQ], F32, name="bias")
         banks = []
         for h in range(2):
@@ -122,7 +117,7 @@ def tile_attend_x_mla_alibi_srt_kernel(tc, qT, cT, ts, pos, slope, ch, offs, out
                 nc.scalar.activation(bias[:, h, j, :], slope_row[:], ACT.Copy, scale=pos_cols[:, h, j : j + 1])
                 nc.tensor.matmul(bank[:, j, :], bias[:, h, j, :], ident[:], start=(j == 0), stop=False, is_transpose=True)
             banks.append(bank)
-        ts_cols = columns(ts_picked, TS_ROW, "ts", "raw")
+        ts_cols = columns(ts_picked, ROW, "ts", "raw")
         gather_low(0)
         turn_values(0)
         gather_low(1)

@@ -80,30 +80,34 @@ def tile_attend_x_mla_alibi_srt_kernel(tc, qT, cT, ts, pos, slope, ch, offs, out
         nc.scalar.copy(slope_row[:], slope_turned[:, 0, :])
 
         low = keep.tile([P, 2, 2, 2, P, 2], BF16, name="low")
-        high = [keep.tile([P, 2, 2, P, 2], BF16, name=f"high{h}") for h in range(2)]
+        high = keep.tile([P, 2, 2, P, 2], BF16, name="high")
         latents = [keep.tile([P, 2, 2, P, PACK], BF16, name=f"latents{h}", align_bytes=64) for h in range(2)]
         values = keep.tile([P, 2, 2, PACK, P // 2, 2], F32, name="values", align_bytes=64)
 
         def picked_pair(t, h):
-            return low[:, :, :, h] if t < 2 else high[h][:]
+            return low[:, :, :, h] if t < 2 else high[:]
 
         def gather_low(t):
             nc.vector.tensor_copy(low[:, t].rearrange("p u h s e -> p (h s) u e"), planes[t][:].indirect(offsets[:]))
 
         def gather_high(t, h):
-            width = PREFIX if h == 0 else T
-            nc.vector.tensor_copy(
-                high[h][:, t - 2].rearrange("p u s e -> p s u e"),
-                planes[t][:, :width].indirect(offsets[:, 32 * h : 32 * (h + 1)]),
-            )
+            if h == 0:
+                nc.vector.tensor_copy(
+                    high[:, t - 2].rearrange("p u s e -> p s u e"), planes[t][:, :PREFIX].indirect(offsets[:, :32])
+                )
+            else:
+                nc.vector.tensor_copy(
+                    latents[1][:, :, :, :, t].rearrange("p u e s -> p s u e"), planes[t][:].indirect(offsets[:, 32:])
+                )
 
         def turn_values(t):
-            turned = psum2.tile([P, 2, 2, P], F32, name="turn")
-            for h in range(2):
+            halves = 2 if t < 2 else 1
+            turned = psum2.tile([P, halves, 2, P], F32, name="turn")
+            for h in range(halves):
                 for u in range(2):
                     words = picked_pair(t, h)[:, t % 2, u].rearrange("p s e -> p (s e)").bitcast(F32)
                     nc.tensor.transpose(turned[:, h, u, :], words, ident[:])
-            nc.scalar.copy(values[:, :, :, t], turned[:].rearrange("s h u (v c) -> s h v c u", v=2))
+            nc.scalar.copy(values[:, :halves, :, t], turned[:].rearrange("s h u (v c) -> s h v c u", v=2))
 
         def interleave(copy, first, h):
             copy(latents[h][:, :, :, :, first : first + 2], picked_pair(first, h).rearrange("p t u s e -> p u e s t"))
@@ -137,15 +141,19 @@ def tile_attend_x_mla_alibi_srt_kernel(tc, qT, cT, ts, pos, slope, ch, offs, out
         for h in range(2):
             gather_high(3, h)
         nc.scalar.copy(q_grouped[:], q_raw[:].rearrange("p t q -> p q t"))
-        interleave(nc.scalar.copy, 2, 0)
+        for part in (slice(0, 16), slice(16, P)):
+            nc.scalar.copy(latents[0][:, :, :, part, 2:], high[:, :, :, part].rearrange("p t u s e -> p u e s t"))
         nc.vector.quantize_mx(
             out=q_codes[:].bitcast(FP8X4), scales=q_scales[:], in_=q_grouped[:].rearrange("p q t -> p (q t)")
         )
-        interleave(nc.vector.tensor_copy, 2, 1)
         turn_values(3)
+        late = psum2.tile([P, PACK, P], F32, name="turn")
+        late_words = latents[1][:].rearrange("p u e s t -> p (u e s t)").bitcast(F32)
+        for j in range(PACK):
+            nc.tensor.transpose(late[:, j, :], late_words[:, 2 * P * j + 1 : 2 * P * (j + 1) : 2], ident[:])
 
-        raws = []
-        for h in range(2):
+        raws = {}
+        for h in (1, 0):
             nc.vector.quantize_mx(
                 out=key_codes[h][:].bitcast(FP8X4),
                 scales=key_scales[h][:],
@@ -163,15 +171,19 @@ def tile_attend_x_mla_alibi_srt_kernel(tc, qT, cT, ts, pos, slope, ch, offs, out
                     start=True,
                     stop=True,
                 )
-            raws.append(raw)
+            raws[h] = raw
 
+        nc.scalar.copy(
+            values[:, 1, :, 2:].bitcast(BF16),
+            late[:].bitcast(BF16).rearrange("s j (v c t) -> s v t c j", v=2, t=2),
+        )
         scaled = [keep.tile([P, PACK, NQ], F32, name=f"scaled{h}") for h in range(2)]
         for j in range(PACK):
-            nc.scalar.activation(scaled[0][:, j, :], raws[0][:, j, :], ACT.Copy, scale=ts_cols[:, 0, j : j + 1])
+            nc.scalar.activation(scaled[1][:, j, :], raws[1][:, j, :], ACT.Copy, scale=ts_cols[:, 1, j : j + 1])
         nc.vector.tensor_tensor(
-            scaled[1][:], raws[1][:], ts_cols[:, 1, :].unsqueeze(2).to_broadcast([P, PACK, NQ]), ALU.mult
+            scaled[0][:], raws[0][:], ts_cols[:, 0, :].unsqueeze(2).to_broadcast([P, PACK, NQ]), ALU.mult
         )
-        for h in range(2):
+        for h in (1, 0):
             for j in range(PACK):
                 nc.tensor.matmul(
                     banks[h][:, j, :], scaled[h][:, j, :], ident[:], start=False, stop=(j == PACK - 1), is_transpose=True
@@ -179,9 +191,9 @@ def tile_attend_x_mla_alibi_srt_kernel(tc, qT, cT, ts, pos, slope, ch, offs, out
 
         negated = keep.tile([NQ, PACK, P], F32, name="val_codes", align_bytes=64)
         floors = keep.tile([NQ, 2], F32, name="floors")
-        nc.vector.tensor_scalar(negated[:], banks[0][:], -1.0, None, ALU.mult, ALU.min, accum_out=floors[:, 0:1])
+        nc.vector.tensor_scalar(negated[:], banks[1][:], -1.0, None, ALU.mult, ALU.min, accum_out=floors[:, 0:1])
         nc.vector.tensor_scalar(
-            negated[:], banks[1][:], -1.0, floors[:, 0:1], ALU.mult, ALU.min, accum_out=floors[:, 1:2]
+            negated[:], banks[0][:], -1.0, floors[:, 0:1], ALU.mult, ALU.min, accum_out=floors[:, 1:2]
         )
 
         val_codes = keep.tile([P, 2, D], U32, name="val_codes", align_bytes=64)

@@ -72,7 +72,7 @@ def tile_attend_x_mla_alibi_srt_kernel(tc, qT, cT, ts, pos, slope, ch, offs, out
 
         nc.vector.memset(posw[:ROW, :], 0.0)
         pos_picked = pick(posw, "pos")
-        nc.gpsimd.memset(tsw[:ROW, :], 0.0)
+        nc.vector.memset(tsw[:ROW, :], 0.0)
         ts_picked = pick(tsw, "ts")
 
         slope_turned = psum1.tile([P, PACK, NQ], F32, name="side0")
@@ -173,10 +173,9 @@ def tile_attend_x_mla_alibi_srt_kernel(tc, qT, cT, ts, pos, slope, ch, offs, out
                 )
             raws[h] = raw
 
-        nc.scalar.copy(
-            values[:, 1, :, 2:].bitcast(BF16),
-            late[:].bitcast(BF16).rearrange("s j (v c t) -> s v t c j", v=2, t=2),
-        )
+        late_values = late[:].bitcast(BF16).rearrange("s j (v c t) -> s v t c j", v=2, t=2)
+        for v, copy in enumerate((nc.scalar.copy, nc.vector.tensor_copy)):
+            copy(values[:, 1, v, 2:].bitcast(BF16), late_values[:, v])
         scaled = [keep.tile([P, PACK, NQ], F32, name=f"scaled{h}") for h in range(2)]
         for j in range(PACK):
             nc.scalar.activation(scaled[1][:, j, :], raws[1][:, j, :], ACT.Copy, scale=ts_cols[:, 1, j : j + 1])
@@ -222,23 +221,25 @@ def tile_attend_x_mla_alibi_srt_kernel(tc, qT, cT, ts, pos, slope, ch, offs, out
 
         w_codes = keep.tile([P, 2, NQ], U32, name="w_codes", align_bytes=64)
         w_scales = keep.tile([P, 2, NQ], U8, name="w_scales", align_bytes=64)
-        weights = []
         for h in range(2):
             turned = psum1.tile([P, PACK, NQ], F32, name=f"side{h}")
             for j in range(PACK):
                 nc.tensor.transpose(turned[:, j, :], probs[:, h, j, :], ident[:])
             w = keep.tile([P, NQ, PACK], BF16, name=f"w{h}", align_bytes=64)
-            nc.vector.tensor_tensor(
-                w[:],
-                turned[:].rearrange("s j q -> s q j"),
-                ts_cols[:, h, :].unsqueeze(1).to_broadcast([P, NQ, PACK]),
-                ALU.mult,
-            )
-            weights.append(w)
-        for h in range(2):
-            nc.vector.quantize_mx(
-                out=w_codes[:, h, :].bitcast(FP8X4), scales=w_scales[:, h, :], in_=weights[h][:].rearrange("s q j -> s (q j)")
-            )
+            parts = (slice(0, NQ // 2), slice(NQ // 2, NQ))
+            for part in parts:
+                nc.vector.tensor_tensor(
+                    w[:, part],
+                    turned[:, :, part].rearrange("s j q -> s q j"),
+                    ts_cols[:, h, :].unsqueeze(1).to_broadcast([P, NQ // 2, PACK]),
+                    ALU.mult,
+                )
+            for part in parts:
+                nc.vector.quantize_mx(
+                    out=w_codes[:, h, part].bitcast(FP8X4),
+                    scales=w_scales[:, h, part],
+                    in_=w[:, part].rearrange("s q j -> s (q j)"),
+                )
         inverse = keep.tile([NQ, 1], F32, name="inverse")
         nc.vector.reciprocal(inverse[:], total[:])
 

@@ -21,33 +21,49 @@ ALU = mybir.AluOpType
 FLOPS = 2 * 2 * NQ * N * D
 BYTES = 4 * (D * T + D * NQ + 2 * T + NQ + D + NQ * D) + 2 * P * N // 16
 
-ROW = 127
+POS_ROWS = slice(0, P, 64)
+TS_ROWS = slice(16, P, 64)
 
 
 def tile_attend_x_mla_alibi_srt_kernel(tc, qT, cT, ts, pos, slope, ch, offs, out):
     nc = tc.nc
     with ExitStack() as ctx:
         keep = ctx.enter_context(tc.tile_pool(name="keep", bufs=1))
+        shared = ctx.enter_context(tc.tile_pool(name="shared", bufs=1))
         psum2 = ctx.enter_context(tc.psum_pool(name="psum2", bufs=2))
         psum1 = ctx.enter_context(tc.psum_pool(name="psum1", bufs=1))
 
         offsets = keep.tile([P, N // 16], U16, name="offsets")
         nc.sync.dma_start(offsets[:], offs)
 
-        planes = [keep.tile([P, T], F32, name=f"plane{t}") for t in range(PACK)]
+        planes = {t: keep.tile([P, T], F32, name=f"plane{t}") for t in (0, 1)}
         tsw = keep.tile([P, T], F32, name="tsw")
-        posw = keep.tile([P, T], F32, name="posw")
+        posw = shared.tile([P, T], F32, name="posw", offset=12 * 1024)
         slope_col = keep.tile([NQ, 1], F32, name="slope_col")
         slope_row = keep.tile([P, NQ], F32, name="slope_row")
-        q_raw = keep.tile([P, PACK, NQ], F32, name="q_raw")
-        ch_sb = keep.tile([P, D], F32, name="ch_sb")
 
         c_view = cT.rearrange("(p t) n -> t p n", t=PACK)
         nc.scalar.dma_start(out=slope_col[:], in_=slope[0])
-        nc.scalar.dma_start(out=posw[ROW:, :], in_=pos[0:1, :])
-        nc.scalar.dma_start(out=tsw[ROW:, :], in_=ts[0:1, :])
-        for t in range(PACK - 1):
+        for t in range(2):
             nc.sync.dma_start(out=planes[t][:], in_=c_view[t])
+        for window, source, rows in ((posw, pos, POS_ROWS), (tsw, ts, TS_ROWS)):
+            nc.vector.memset(window[:], 0.0)
+            for piece, row in enumerate(range(P)[rows]):
+                tokens = slice(T // 2 * piece, T // 2 * (piece + 1))
+                nc.scalar.dma_start(out=window[row : row + 1, tokens], in_=source[0:1, tokens])
+
+        def pick(window, label):
+            picked = keep.tile([P, N], F32, name=f"{label}_picked")
+            nc.vector.tensor_copy(picked[:], window[:].indirect(offsets[:]))
+            return picked
+
+        pos_picked = pick(posw, "pos")
+        ts_picked = pick(tsw, "ts")
+        planes[3] = shared.tile([P, T], F32, name="plane3", offset=0)
+        q_raw = shared.tile([P, PACK, NQ], F32, name="q_raw", offset=16 * 1024)
+        ch_sb = shared.tile([P, D], F32, name="ch_sb", offset=18 * 1024)
+        planes[2] = shared.tile([P, T], F32, name="plane2", offset=20 * 1024)
+        nc.sync.dma_start(out=planes[2][:], in_=c_view[2])
         nc.sync.dma_start(out=planes[3][:, :PREFIX], in_=c_view[3][:, :PREFIX])
         nc.sync.dma_start(out=q_raw[:], in_=qT[0].rearrange("(p t) q -> p t q", t=PACK))
         nc.sync.dma_start(out=planes[3][:, PREFIX:], in_=c_view[3][:, PREFIX:])
@@ -56,30 +72,22 @@ def tile_attend_x_mla_alibi_srt_kernel(tc, qT, cT, ts, pos, slope, ch, offs, out
         ident = keep.tile([P, P], F32, name="ident")
         make_identity(nc, ident[:])
 
-        def pick(window, label):
-            picked = keep.tile([P, N], F32, name=f"{label}_picked")
-            nc.vector.tensor_copy(picked[:], window[:].indirect(offsets[:]))
-            return picked
-
-        def columns(picked, row, label, bank_name):
+        def columns(picked, rows, label, bank_name):
             cols = keep.tile([P, 2, PACK], F32, name=f"{label}_cols")
+            both = keep.tile([P, 2, PACK, 2], F32, name=f"{label}_both")
             for h in range(2):
                 turned = psum1.tile([P, PACK, P], F32, name=f"{bank_name}{h}")
                 for j in range(PACK):
                     nc.tensor.transpose(turned[:, j, :], picked[:, HALF * h + j : HALF * (h + 1) : PACK], ident[:])
-                nc.scalar.copy(cols[:, h, :], turned[:, :, row])
+                for j in range(PACK):
+                    nc.scalar.activation(both[:, h, j], turned[:, j, rows], ACT.Copy, accum_out=cols[:, h, j : j + 1])
             return cols
-
-        nc.vector.memset(posw[:ROW, :], 0.0)
-        pos_picked = pick(posw, "pos")
-        nc.vector.memset(tsw[:ROW, :], 0.0)
-        ts_picked = pick(tsw, "ts")
 
         slope_turned = psum1.tile([P, PACK, NQ], F32, name="side0")
         nc.tensor.transpose(slope_turned[:, 0, :], slope_col[:].to_broadcast([NQ, P]), ident[:])
         nc.scalar.copy(slope_row[:], slope_turned[:, 0, :])
 
-        low = keep.tile([P, 2, 2, 2, P, 2], BF16, name="low")
+        low = keep.tile([P, 2, 2, 2, P, 2], BF16, name="tsw")
         high = keep.tile([P, 2, 2, P, 2], BF16, name="high")
         latents = [keep.tile([P, 2, 2, P, PACK], BF16, name=f"latents{h}", align_bytes=64) for h in range(2)]
         values = keep.tile([P, 2, 2, PACK, P // 2, 2], F32, name="values", align_bytes=64)
@@ -112,7 +120,7 @@ def tile_attend_x_mla_alibi_srt_kernel(tc, qT, cT, ts, pos, slope, ch, offs, out
         def interleave(copy, first, h):
             copy(latents[h][:, :, :, :, first : first + 2], picked_pair(first, h).rearrange("p t u s e -> p u e s t"))
 
-        pos_cols = columns(pos_picked, ROW, "pos", "side")
+        pos_cols = columns(pos_picked, POS_ROWS, "pos", "side")
         bias = keep.tile([P, 2, PACK, NQ], F32, name="bias")
         banks = []
         for h in range(2):
@@ -121,7 +129,7 @@ def tile_attend_x_mla_alibi_srt_kernel(tc, qT, cT, ts, pos, slope, ch, offs, out
                 nc.scalar.activation(bias[:, h, j, :], slope_row[:], ACT.Copy, scale=pos_cols[:, h, j : j + 1])
                 nc.tensor.matmul(bank[:, j, :], bias[:, h, j, :], ident[:], start=(j == 0), stop=False, is_transpose=True)
             banks.append(bank)
-        ts_cols = columns(ts_picked, ROW, "ts", "raw")
+        ts_cols = columns(ts_picked, TS_ROWS, "ts", "raw")
         gather_low(0)
         turn_values(0)
         gather_low(1)

@@ -21,7 +21,7 @@ ALU = mybir.AluOpType
 FLOPS = 2 * 2 * NQ * N * D
 BYTES = 4 * (D * T + D * NQ + 2 * T + NQ + D + NQ * D) + 2 * P * N // 16
 
-POS_ROWS = slice(0, P, 64)
+POS_ROWS = slice(0, P, P - 1)
 TS_ROWS = slice(16, P, 64)
 
 
@@ -43,13 +43,13 @@ def tile_attend_x_mla_alibi_srt_kernel(tc, qT, cT, ts, pos, slope, ch, offs, out
         slope_row = keep.tile([P, NQ], F32, name="slope_row")
 
         c_view = cT.rearrange("(p t) n -> t p n", t=PACK)
-        nc.scalar.dma_start(out=slope_col[:], in_=slope[0])
-        for t in range(2):
-            nc.sync.dma_start(out=planes[t][:], in_=c_view[t])
+        nc.sync.dma_start(out=planes[0][:], in_=c_view[0])
+        nc.sync.dma_start(out=slope_col[:], in_=slope[0])
+        nc.sync.dma_start(out=planes[1][:], in_=c_view[1])
         for window, source, rows in ((posw, pos, POS_ROWS), (tsw, ts, TS_ROWS)):
-            nc.vector.memset(window[:], 0.0)
             for piece, row in enumerate(range(P)[rows]):
                 tokens = slice(T // 2 * piece, T // 2 * (piece + 1))
+                nc.vector.memset(window[: row if row == P - 1 else P, tokens], 0.0)
                 nc.scalar.dma_start(out=window[row : row + 1, tokens], in_=source[0:1, tokens])
 
         def pick(window, label):
@@ -58,11 +58,10 @@ def tile_attend_x_mla_alibi_srt_kernel(tc, qT, cT, ts, pos, slope, ch, offs, out
             return picked
 
         pos_picked = pick(posw, "pos")
-        ts_picked = pick(tsw, "ts")
         planes[3] = shared.tile([P, T], F32, name="plane3", offset=0)
         q_raw = shared.tile([P, PACK, NQ], F32, name="q_raw", offset=16 * 1024)
         ch_sb = shared.tile([P, D], F32, name="ch_sb", offset=18 * 1024)
-        planes[2] = shared.tile([P, T], F32, name="plane2", offset=20 * 1024)
+        planes[2] = shared.tile([P, T], F32, name="plane2", offset=24 * 1024)
         nc.sync.dma_start(out=planes[2][:], in_=c_view[2])
         nc.sync.dma_start(out=planes[3][:, :PREFIX], in_=c_view[3][:, :PREFIX])
         nc.sync.dma_start(out=q_raw[:], in_=qT[0].rearrange("(p t) q -> p t q", t=PACK))
@@ -87,7 +86,7 @@ def tile_attend_x_mla_alibi_srt_kernel(tc, qT, cT, ts, pos, slope, ch, offs, out
         nc.tensor.transpose(slope_turned[:, 0, :], slope_col[:].to_broadcast([NQ, P]), ident[:])
         nc.scalar.copy(slope_row[:], slope_turned[:, 0, :])
 
-        low = keep.tile([P, 2, 2, 2, P, 2], BF16, name="tsw")
+        low = shared.tile([P, 2, 2, 2, P, 2], BF16, name="low", offset=20 * 1024)
         high = keep.tile([P, 2, 2, P, 2], BF16, name="high")
         latents = [keep.tile([P, 2, 2, P, PACK], BF16, name=f"latents{h}", align_bytes=64) for h in range(2)]
         values = keep.tile([P, 2, 2, PACK, P // 2, 2], F32, name="values", align_bytes=64)
@@ -129,15 +128,15 @@ def tile_attend_x_mla_alibi_srt_kernel(tc, qT, cT, ts, pos, slope, ch, offs, out
                 nc.scalar.activation(bias[:, h, j, :], slope_row[:], ACT.Copy, scale=pos_cols[:, h, j : j + 1])
                 nc.tensor.matmul(bank[:, j, :], bias[:, h, j, :], ident[:], start=(j == 0), stop=False, is_transpose=True)
             banks.append(bank)
-        ts_cols = columns(ts_picked, TS_ROWS, "ts", "raw")
         gather_low(0)
         turn_values(0)
+        ts_cols = columns(pick(tsw, "ts"), TS_ROWS, "ts", "raw")
         gather_low(1)
         turn_values(1)
         interleave(nc.scalar.copy, 0, 0)
+        interleave(nc.vector.tensor_copy, 0, 1)
         for h in range(2):
             gather_high(2, h)
-        interleave(nc.vector.tensor_copy, 0, 1)
         turn_values(2)
 
         key_codes = [keep.tile([P, HALF], U32, name=f"key_codes{h}", align_bytes=64) for h in range(2)]

@@ -147,9 +147,8 @@ def tile_attend_x_mla_alibi_srt_kernel(tc, qT, cT, ts, pos, slope, ch, offs, out
 
         for h in range(2):
             gather_high(3, h)
-        nc.scalar.copy(q_grouped[:], q_raw[:].rearrange("p t q -> p q t"))
-        for part in (slice(0, 16), slice(16, P)):
-            nc.scalar.copy(latents[0][:, :, :, part, 2:], high[:, :, :, part].rearrange("p t u s e -> p u e s t"))
+        nc.gpsimd.tensor_copy(q_grouped[:], q_raw[:].rearrange("p t q -> p q t"))
+        interleave(nc.scalar.copy, 2, 0)
         nc.vector.quantize_mx(
             out=q_codes[:].bitcast(FP8X4), scales=q_scales[:], in_=q_grouped[:].rearrange("p q t -> p (q t)")
         )

@@ -87,20 +87,23 @@ def tile_attend_x_mla_alibi_srt_kernel(tc, qT, cT, ts, pos, slope, ch, offs, out
         nc.scalar.copy(slope_row[:], slope_turned[:, 0, :])
 
         low = shared.tile([P, 2, 2, 2, P, 2], BF16, name="low", offset=20 * 1024)
-        high = keep.tile([P, 2, 2, P, 2], BF16, name="high")
+        high = keep.tile([P, 2, 2, 2, P, 2], BF16, name="high")
         latents = [keep.tile([P, 2, 2, P, PACK], BF16, name=f"latents{h}", align_bytes=64) for h in range(2)]
         values = keep.tile([P, 2, 2, PACK, P // 2, 2], F32, name="values", align_bytes=64)
 
         def picked_pair(t, h):
-            return low[:, :, :, h] if t < 2 else high[:]
+            return (low if t < 2 else high)[:, :, :, h]
 
-        def gather_low(t):
-            nc.vector.tensor_copy(low[:, t].rearrange("p u h s e -> p (h s) u e"), planes[t][:].indirect(offsets[:]))
+        def gather_whole(t):
+            picked = low if t < 2 else high
+            nc.vector.tensor_copy(
+                picked[:, t % 2].rearrange("p u h s e -> p (h s) u e"), planes[t][:].indirect(offsets[:])
+            )
 
         def gather_high(t, h):
             if h == 0:
                 nc.vector.tensor_copy(
-                    high[:, t - 2].rearrange("p u s e -> p s u e"), planes[t][:, :PREFIX].indirect(offsets[:, :32])
+                    high[:, t - 2, :, 0].rearrange("p u s e -> p s u e"), planes[t][:, :PREFIX].indirect(offsets[:, :32])
                 )
             else:
                 nc.vector.tensor_copy(
@@ -108,7 +111,7 @@ def tile_attend_x_mla_alibi_srt_kernel(tc, qT, cT, ts, pos, slope, ch, offs, out
                 )
 
         def turn_values(t):
-            halves = 2 if t < 2 else 1
+            halves = 2 if t < 3 else 1
             turned = psum2.tile([P, halves, 2, P], F32, name="turn")
             for h in range(halves):
                 for u in range(2):
@@ -128,15 +131,15 @@ def tile_attend_x_mla_alibi_srt_kernel(tc, qT, cT, ts, pos, slope, ch, offs, out
                 nc.scalar.activation(bias[:, h, j, :], slope_row[:], ACT.Copy, scale=pos_cols[:, h, j : j + 1])
                 nc.tensor.matmul(bank[:, j, :], bias[:, h, j, :], ident[:], start=(j == 0), stop=False, is_transpose=True)
             banks.append(bank)
-        gather_low(0)
+        gather_whole(0)
         turn_values(0)
         ts_cols = columns(pick(tsw, "ts"), TS_ROWS, "ts", "raw")
-        gather_low(1)
+        gather_whole(1)
         turn_values(1)
         interleave(nc.scalar.copy, 0, 0)
         interleave(nc.vector.tensor_copy, 0, 1)
-        for h in range(2):
-            gather_high(2, h)
+        gather_whole(2)
+        nc.vector.tensor_copy(latents[1][:, :, :, :, 2], high[:, 0, :, 1].rearrange("p u s e -> p u e s"))
         turn_values(2)
 
         key_codes = [keep.tile([P, HALF], U32, name=f"key_codes{h}", align_bytes=64) for h in range(2)]
@@ -153,10 +156,6 @@ def tile_attend_x_mla_alibi_srt_kernel(tc, qT, cT, ts, pos, slope, ch, offs, out
             out=q_codes[:].bitcast(FP8X4), scales=q_scales[:], in_=q_grouped[:].rearrange("p q t -> p (q t)")
         )
         turn_values(3)
-        late = psum2.tile([P, PACK, P], F32, name="turn")
-        late_words = latents[1][:].rearrange("p u e s t -> p (u e s t)").bitcast(F32)
-        for j in range(PACK):
-            nc.tensor.transpose(late[:, j, :], late_words[:, 2 * P * j + 1 : 2 * P * (j + 1) : 2], ident[:])
 
         raws = {}
         for h in (1, 0):
@@ -179,9 +178,20 @@ def tile_attend_x_mla_alibi_srt_kernel(tc, qT, cT, ts, pos, slope, ch, offs, out
                 )
             raws[h] = raw
 
-        late_values = late[:].bitcast(BF16).rearrange("s j (v c t) -> s v t c j", v=2, t=2)
-        for v, copy in enumerate((nc.scalar.copy, nc.vector.tensor_copy)):
-            copy(values[:, 1, v, 2:].bitcast(BF16), late_values[:, v])
+        val_codes = [
+            shared.tile([P, D], U32, name="val_codes0", offset=0, align_bytes=64),
+            keep.tile([P, D], U32, name="val_codes1", align_bytes=64),
+        ]
+        val_scales = keep.tile([P, 2, D], U8, name="val_scales", align_bytes=64)
+
+        def quantise_values(h):
+            nc.vector.quantize_mx(
+                out=val_codes[h][:].bitcast(FP8X4),
+                scales=val_scales[:, h, :],
+                in_=values[:, h].rearrange("s v t c u -> s (v t c u)").bitcast(BF16),
+            )
+
+        quantise_values(0)
         scaled = [keep.tile([P, PACK, NQ], F32, name=f"scaled{h}") for h in range(2)]
         for j in range(PACK):
             nc.scalar.activation(scaled[1][:, j, :], raws[1][:, j, :], ACT.Copy, scale=ts_cols[:, 1, j : j + 1])
@@ -194,21 +204,21 @@ def tile_attend_x_mla_alibi_srt_kernel(tc, qT, cT, ts, pos, slope, ch, offs, out
                     banks[h][:, j, :], scaled[h][:, j, :], ident[:], start=False, stop=(j == PACK - 1), is_transpose=True
                 )
 
-        negated = keep.tile([NQ, PACK, P], F32, name="val_codes", align_bytes=64)
+        late = psum1.tile([P, PACK, P], F32, name="raw0")
+        late_words = latents[1][:].rearrange("p u e s t -> p (u e s t)").bitcast(F32)
+        for j in range(PACK):
+            nc.tensor.transpose(late[:, j, :], late_words[:, 2 * P * j + 1 : 2 * P * (j + 1) : 2], ident[:])
+
+        negated = keep.tile([NQ, PACK, P], F32, name="negated")
         floors = keep.tile([NQ, 2], F32, name="floors")
         nc.vector.tensor_scalar(negated[:], banks[1][:], -1.0, None, ALU.mult, ALU.min, accum_out=floors[:, 0:1])
         nc.vector.tensor_scalar(
             negated[:], banks[0][:], -1.0, floors[:, 0:1], ALU.mult, ALU.min, accum_out=floors[:, 1:2]
         )
 
-        val_codes = keep.tile([P, 2, D], U32, name="val_codes", align_bytes=64)
-        val_scales = keep.tile([P, 2, D], U8, name="val_scales", align_bytes=64)
-        for h in range(2):
-            nc.vector.quantize_mx(
-                out=val_codes[:, h, :].bitcast(FP8X4),
-                scales=val_scales[:, h, :],
-                in_=values[:, h].rearrange("s v t c u -> s (v t c u)").bitcast(BF16),
-            )
+        late_values = late[:].bitcast(BF16).rearrange("s j (v c t) -> s v t c j", v=2, t=2)
+        nc.vector.tensor_copy(values[:, 1, :, 3].bitcast(BF16), late_values[:, :, 1])
+        quantise_values(1)
 
         probs = keep.tile([NQ, 2, PACK, P], F32, name="probs")
         sums = keep.tile([NQ, 4], F32, name="sums")
@@ -257,7 +267,7 @@ def tile_attend_x_mla_alibi_srt_kernel(tc, qT, cT, ts, pos, slope, ch, offs, out
                     out=outputs[v][:],
                     lhsT=w_codes[:, h, :].bitcast(FP8X4),
                     lhsT_scale=w_scales[:, h, :],
-                    rhs=val_codes[:, h, cols].bitcast(FP8X4),
+                    rhs=val_codes[h][:, cols].bitcast(FP8X4),
                     rhs_scale=val_scales[:, h, cols],
                     start=(h == 0),
                     stop=(h == 1),

@@ -157,18 +157,25 @@ def tile_attend_x_mla_alibi_srt_kernel(tc, qT, cT, ts, pos, slope, ch, offs, out
         )
         turn_values(3)
 
-        raws = {}
-        for h in (1, 0):
+        late = psum2.tile([P, PACK, P], F32, name="turn")
+        late_words = latents[1][:].rearrange("p u e s t -> p (u e s t)").bitcast(F32)
+        for j in range(PACK):
+            nc.tensor.transpose(late[:, j, :], late_words[:, 2 * P * j + 1 : 2 * P * (j + 1) : 2], ident[:])
+        late_values = late[:].bitcast(BF16).rearrange("s j (v c t) -> s v t c j", v=2, t=2)
+        nc.scalar.copy(values[:, 1, :, 3].bitcast(BF16), late_values[:, :, 1])
+
+        def scores(h, blocks, bank_name):
+            cols = slice(P * blocks[0], P * (blocks[-1] + 1))
             nc.vector.quantize_mx(
-                out=key_codes[h][:].bitcast(FP8X4),
-                scales=key_scales[h][:],
-                in_=latents[h][:].rearrange("p u e s t -> p (u e s t)"),
+                out=key_codes[h][:, cols].bitcast(FP8X4),
+                scales=key_scales[h][:, cols],
+                in_=latents[h][:].rearrange("p u e s t -> p (u e s t)")[:, PACK * cols.start : PACK * cols.stop],
             )
-            raw = psum1.tile([P, PACK, NQ], F32, name=f"raw{h}")
-            for j in range(PACK):
+            raw = psum1.tile([P, len(blocks), NQ], F32, name=bank_name)
+            for i, j in enumerate(blocks):
                 block = slice(P * j, P * (j + 1))
                 nc.tensor.matmul_mx(
-                    out=raw[:, j, :],
+                    out=raw[:, i, :],
                     lhsT=key_codes[h][:, block].bitcast(FP8X4),
                     lhsT_scale=key_scales[h][:, block],
                     rhs=q_codes[:].bitcast(FP8X4),
@@ -176,49 +183,44 @@ def tile_attend_x_mla_alibi_srt_kernel(tc, qT, cT, ts, pos, slope, ch, offs, out
                     start=True,
                     stop=True,
                 )
-            raws[h] = raw
+            return raw
 
-        val_codes = [
-            shared.tile([P, D], U32, name="val_codes0", offset=0, align_bytes=64),
-            keep.tile([P, D], U32, name="val_codes1", align_bytes=64),
-        ]
-        val_scales = keep.tile([P, 2, D], U8, name="val_scales", align_bytes=64)
-
-        def quantise_values(h):
-            nc.vector.quantize_mx(
-                out=val_codes[h][:].bitcast(FP8X4),
-                scales=val_scales[:, h, :],
-                in_=values[:, h].rearrange("s v t c u -> s (v t c u)").bitcast(BF16),
-            )
-
-        quantise_values(0)
+        raws = {
+            (h, u): scores(h, range(2 * u, 2 * u + 2), name)
+            for (h, u), name in zip(((1, 0), (1, 1), (0, 0), (0, 1)), ("side0", "raw1", "side1", "raw0"))
+        }
         scaled = [keep.tile([P, PACK, NQ], F32, name=f"scaled{h}") for h in range(2)]
-        for j in range(PACK):
-            nc.scalar.activation(scaled[1][:, j, :], raws[1][:, j, :], ACT.Copy, scale=ts_cols[:, 1, j : j + 1])
-        nc.vector.tensor_tensor(
-            scaled[0][:], raws[0][:], ts_cols[:, 0, :].unsqueeze(2).to_broadcast([P, PACK, NQ]), ALU.mult
-        )
         for h in (1, 0):
-            for j in range(PACK):
+            for j in range(2):
+                nc.scalar.activation(scaled[h][:, j, :], raws[h, 0][:, j, :], ACT.Copy, scale=ts_cols[:, h, j : j + 1])
+            nc.vector.tensor_tensor(
+                scaled[h][:, 2:], raws[h, 1][:], ts_cols[:, h, 2:].unsqueeze(2).to_broadcast([P, 2, NQ]), ALU.mult
+            )
+        for h, blocks in ((1, (0, 1, 2, 3)), (0, (0, 1, 2, 3))):
+            for j in blocks:
                 nc.tensor.matmul(
-                    banks[h][:, j, :], scaled[h][:, j, :], ident[:], start=False, stop=(j == PACK - 1), is_transpose=True
+                    banks[h][:, j, :], scaled[h][:, j, :], ident[:], start=False, stop=(j == blocks[-1]), is_transpose=True
                 )
 
-        late = psum1.tile([P, PACK, P], F32, name="raw0")
-        late_words = latents[1][:].rearrange("p u e s t -> p (u e s t)").bitcast(F32)
-        for j in range(PACK):
-            nc.tensor.transpose(late[:, j, :], late_words[:, 2 * P * j + 1 : 2 * P * (j + 1) : 2], ident[:])
-
-        negated = keep.tile([NQ, PACK, P], F32, name="negated")
+        negated = keep.tile([NQ, PACK, P], F32, name="val_codes", align_bytes=64)
         floors = keep.tile([NQ, 2], F32, name="floors")
         nc.vector.tensor_scalar(negated[:], banks[1][:], -1.0, None, ALU.mult, ALU.min, accum_out=floors[:, 0:1])
         nc.vector.tensor_scalar(
             negated[:], banks[0][:], -1.0, floors[:, 0:1], ALU.mult, ALU.min, accum_out=floors[:, 1:2]
         )
 
-        late_values = late[:].bitcast(BF16).rearrange("s j (v c t) -> s v t c j", v=2, t=2)
-        nc.vector.tensor_copy(values[:, 1, :, 3].bitcast(BF16), late_values[:, :, 1])
-        quantise_values(1)
+        val_codes = keep.tile([P, 2, D], U32, name="val_codes", align_bytes=64)
+        val_scales = keep.tile([P, 2, D], U8, name="val_scales", align_bytes=64)
+
+        def quantise_values(h):
+            nc.vector.quantize_mx(
+                out=val_codes[:, h, :].bitcast(FP8X4),
+                scales=val_scales[:, h, :],
+                in_=values[:, h].rearrange("s v t c u -> s (v t c u)").bitcast(BF16),
+            )
+
+        for h in range(2):
+            quantise_values(h)
 
         probs = keep.tile([NQ, 2, PACK, P], F32, name="probs")
         sums = keep.tile([NQ, 4], F32, name="sums")
@@ -237,25 +239,34 @@ def tile_attend_x_mla_alibi_srt_kernel(tc, qT, cT, ts, pos, slope, ch, offs, out
 
         w_codes = keep.tile([P, 2, NQ], U32, name="w_codes", align_bytes=64)
         w_scales = keep.tile([P, 2, NQ], U8, name="w_scales", align_bytes=64)
+        w = [keep.tile([P, NQ, PACK], BF16, name=f"w{h}", align_bytes=64) for h in range(2)]
+        turned = [psum1.tile([P, PACK, NQ], F32, name=f"side{h}") for h in range(2)]
         for h in range(2):
-            turned = psum1.tile([P, PACK, NQ], F32, name=f"side{h}")
             for j in range(PACK):
-                nc.tensor.transpose(turned[:, j, :], probs[:, h, j, :], ident[:])
-            w = keep.tile([P, NQ, PACK], BF16, name=f"w{h}", align_bytes=64)
-            parts = (slice(0, NQ // 2), slice(NQ // 2, NQ))
-            for part in parts:
-                nc.vector.tensor_tensor(
-                    w[:, part],
-                    turned[:, :, part].rearrange("s j q -> s q j"),
-                    ts_cols[:, h, :].unsqueeze(1).to_broadcast([P, NQ // 2, PACK]),
-                    ALU.mult,
-                )
-            for part in parts:
-                nc.vector.quantize_mx(
-                    out=w_codes[:, h, part].bitcast(FP8X4),
-                    scales=w_scales[:, h, part],
-                    in_=w[:, part].rearrange("s q j -> s (q j)"),
-                )
+                nc.tensor.transpose(turned[h][:, j, :], probs[:, h, j, :], ident[:])
+
+        def weigh(h, part):
+            nc.vector.tensor_tensor(
+                w[h][:, part],
+                turned[h][:, :, part].rearrange("s j q -> s q j"),
+                ts_cols[:, h, :].unsqueeze(1).to_broadcast([P, part.stop - part.start, PACK]),
+                ALU.mult,
+            )
+
+        def quantise_weights(h, part):
+            nc.vector.quantize_mx(
+                out=w_codes[:, h, part].bitcast(FP8X4),
+                scales=w_scales[:, h, part],
+                in_=w[h][:, part].rearrange("s q j -> s (q j)"),
+            )
+
+        parts = (slice(0, NQ // 2), slice(NQ // 2, NQ))
+        weigh(0, slice(0, NQ))
+        weigh(1, parts[0])
+        quantise_weights(0, slice(0, NQ))
+        weigh(1, parts[1])
+        for part in parts:
+            quantise_weights(1, part)
         inverse = keep.tile([NQ, 1], F32, name="inverse")
         nc.vector.reciprocal(inverse[:], total[:])
 
@@ -267,7 +278,7 @@ def tile_attend_x_mla_alibi_srt_kernel(tc, qT, cT, ts, pos, slope, ch, offs, out
                     out=outputs[v][:],
                     lhsT=w_codes[:, h, :].bitcast(FP8X4),
                     lhsT_scale=w_scales[:, h, :],
-                    rhs=val_codes[h][:, cols].bitcast(FP8X4),
+                    rhs=val_codes[:, h, cols].bitcast(FP8X4),
                     rhs_scale=val_scales[:, h, cols],
                     start=(h == 0),
                     stop=(h == 1),

@@ -8,6 +8,7 @@ P = 128
 PACK = 4
 HALF = 512
 PREFIX = T - HALF
+PIECES = 4
 
 F32 = mybir.dt.float32
 BF16 = mybir.dt.bfloat16
@@ -30,7 +31,7 @@ def tile_attend_x_mla_alibi_srt_kernel(tc, qT, cT, ts, pos, slope, ch, offs, out
     with ExitStack() as ctx:
         keep = ctx.enter_context(tc.tile_pool(name="keep", bufs=1))
         shared = ctx.enter_context(tc.tile_pool(name="shared", bufs=1))
-        psum2 = ctx.enter_context(tc.psum_pool(name="psum2", bufs=2))
+        psum2 = ctx.enter_context(tc.psum_pool(name="psum2", bufs=1))
         psum1 = ctx.enter_context(tc.psum_pool(name="psum1", bufs=1))
 
         offsets = keep.tile([P, N // 16], U16, name="offsets")
@@ -84,12 +85,12 @@ def tile_attend_x_mla_alibi_srt_kernel(tc, qT, cT, ts, pos, slope, ch, offs, out
 
         slope_turned = psum1.tile([P, PACK, NQ], F32, name="side0")
         nc.tensor.transpose(slope_turned[:, 0, :], slope_col[:].to_broadcast([NQ, P]), ident[:])
-        nc.scalar.copy(slope_row[:], slope_turned[:, 0, :])
+        nc.scalar.activation(slope_row[:], slope_turned[:, 0, :], ACT.Copy, scale=-1.0)
 
         low = shared.tile([P, 2, 2, 2, P, 2], BF16, name="low", offset=20 * 1024)
         high = keep.tile([P, 2, 2, 2, P, 2], BF16, name="high")
         latents = [keep.tile([P, 2, 2, P, PACK], BF16, name=f"latents{h}", align_bytes=64) for h in range(2)]
-        values = keep.tile([P, 2, 2, PACK, P // 2, 2], F32, name="values", align_bytes=64)
+        values = keep.tile([P, 2, PIECES, PACK, P // PIECES, 2], F32, name="values", align_bytes=64)
 
         def picked_pair(t, h):
             return (low if t < 2 else high)[:, :, :, h]
@@ -112,28 +113,37 @@ def tile_attend_x_mla_alibi_srt_kernel(tc, qT, cT, ts, pos, slope, ch, offs, out
 
         def turn_values(t):
             halves = 2 if t < 3 else 1
-            turned = psum2.tile([P, halves, 2, P], F32, name="turn")
+            turned = psum2.tile([P, 2, 2, P], F32, name="turn") if t < 3 else psum1.tile([P, 1, 2, P], F32, name="raw0")
             for h in range(halves):
                 for u in range(2):
                     words = picked_pair(t, h)[:, t % 2, u].rearrange("p s e -> p (s e)").bitcast(F32)
                     nc.tensor.transpose(turned[:, h, u, :], words, ident[:])
-            nc.scalar.copy(values[:, :halves, :, t], turned[:].rearrange("s h u (v c) -> s h v c u", v=2))
+            nc.scalar.copy(values[:, :halves, :, t], turned[:].rearrange("s h u (v c) -> s h v c u", v=PIECES))
 
         def interleave(copy, first, h):
             copy(latents[h][:, :, :, :, first : first + 2], picked_pair(first, h).rearrange("p t u s e -> p u e s t"))
 
         pos_cols = columns(pos_picked, POS_ROWS, "pos", "side")
         bias = keep.tile([P, 2, PACK, NQ], F32, name="bias")
-        banks = []
+        banks = [
+            psum1.tile([NQ, PACK, P], F32, name="scores0"),
+            psum1.tile([NQ, 2, P], F32, name="scores1"),
+            psum1.tile([NQ, 2, P], F32, name="scores2"),
+        ]
+
+        def score_block(h, j):
+            return banks[0][:, j, :] if h == 0 else banks[1 + j // 2][:, j % 2, :]
+
         for h in range(2):
-            bank = psum1.tile([NQ, PACK, P], F32, name=f"scores{h}")
             for j in range(PACK):
                 nc.scalar.activation(bias[:, h, j, :], slope_row[:], ACT.Copy, scale=pos_cols[:, h, j : j + 1])
-                nc.tensor.matmul(bank[:, j, :], bias[:, h, j, :], ident[:], start=(j == 0), stop=False, is_transpose=True)
-            banks.append(bank)
+                first = j == 0 or (h == 1 and j == 2)
+                nc.tensor.matmul(score_block(h, j), bias[:, h, j, :], ident[:], start=first, stop=False, is_transpose=True)
         gather_whole(0)
         turn_values(0)
         ts_cols = columns(pick(tsw, "ts"), TS_ROWS, "ts", "raw")
+        minus_ts = keep.tile([P, 2, PACK], F32, name="minus_ts")
+        nc.scalar.activation(minus_ts[:], ts_cols[:], ACT.Copy, scale=-1.0)
         gather_whole(1)
         turn_values(1)
         interleave(nc.scalar.copy, 0, 0)
@@ -161,7 +171,7 @@ def tile_attend_x_mla_alibi_srt_kernel(tc, qT, cT, ts, pos, slope, ch, offs, out
         late_words = latents[1][:].rearrange("p u e s t -> p (u e s t)").bitcast(F32)
         for j in range(PACK):
             nc.tensor.transpose(late[:, j, :], late_words[:, 2 * P * j + 1 : 2 * P * (j + 1) : 2], ident[:])
-        late_values = late[:].bitcast(BF16).rearrange("s j (v c t) -> s v t c j", v=2, t=2)
+        late_values = late[:].bitcast(BF16).rearrange("s j (v c t) -> s v t c j", v=PIECES, t=2)
         nc.scalar.copy(values[:, 1, :, 3].bitcast(BF16), late_values[:, :, 1])
 
         def scores(h, blocks, bank_name):
@@ -191,59 +201,72 @@ def tile_attend_x_mla_alibi_srt_kernel(tc, qT, cT, ts, pos, slope, ch, offs, out
         }
         scaled = [keep.tile([P, PACK, NQ], F32, name=f"scaled{h}") for h in range(2)]
         for h in (1, 0):
-            for j in range(2):
-                nc.scalar.activation(scaled[h][:, j, :], raws[h, 0][:, j, :], ACT.Copy, scale=ts_cols[:, h, j : j + 1])
-            nc.vector.tensor_tensor(
-                scaled[h][:, 2:], raws[h, 1][:], ts_cols[:, h, 2:].unsqueeze(2).to_broadcast([P, 2, NQ]), ALU.mult
-            )
-        for h, blocks in ((1, (0, 1, 2, 3)), (0, (0, 1, 2, 3))):
-            for j in blocks:
-                nc.tensor.matmul(
-                    banks[h][:, j, :], scaled[h][:, j, :], ident[:], start=False, stop=(j == blocks[-1]), is_transpose=True
-                )
-
-        negated = keep.tile([NQ, PACK, P], F32, name="val_codes", align_bytes=64)
-        floors = keep.tile([NQ, 2], F32, name="floors")
-        nc.vector.tensor_scalar(negated[:], banks[1][:], -1.0, None, ALU.mult, ALU.min, accum_out=floors[:, 0:1])
-        nc.vector.tensor_scalar(
-            negated[:], banks[0][:], -1.0, floors[:, 0:1], ALU.mult, ALU.min, accum_out=floors[:, 1:2]
-        )
-
-        val_codes = keep.tile([P, 2, D], U32, name="val_codes", align_bytes=64)
-        val_scales = keep.tile([P, 2, D], U8, name="val_scales", align_bytes=64)
-
-        def quantise_values(h):
-            nc.vector.quantize_mx(
-                out=val_codes[:, h, :].bitcast(FP8X4),
-                scales=val_scales[:, h, :],
-                in_=values[:, h].rearrange("s v t c u -> s (v t c u)").bitcast(BF16),
-            )
-
-        for h in range(2):
-            quantise_values(h)
-
-        probs = keep.tile([NQ, 2, PACK, P], F32, name="probs")
-        sums = keep.tile([NQ, 4], F32, name="sums")
-        for h in range(2):
-            for u in range(2):
+            for j in range(PACK):
                 nc.scalar.activation(
-                    probs[:, h, 2 * u : 2 * u + 2],
-                    banks[h][:, 2 * u : 2 * u + 2],
-                    ACT.Exp,
-                    bias=floors[:, 1:2],
-                    accum_out=sums[:, 2 * h + u : 2 * h + u + 1],
+                    scaled[h][:, j, :], raws[h, j // 2][:, j % 2, :], ACT.Copy, scale=minus_ts[:, h, j : j + 1]
                 )
-        sums_copy = keep.tile([NQ, 4], F32, name="sums_copy")
-        total = keep.tile([NQ, 1], F32, name="total")
-        nc.scalar.activation(sums_copy[:], sums[:], ACT.Copy, accum_out=total[:])
+        for h in (1, 0):
+            for j in range(PACK):
+                last = j == 3 or (h == 1 and j == 1)
+                nc.tensor.matmul(score_block(h, j), scaled[h][:, j, :], ident[:], start=False, stop=last, is_transpose=True)
 
+        spare = keep.tile([NQ, 2, PACK, P], F32, name="spare")
+        floors = keep.tile([NQ, 3], F32, name="floors")
+        probs = keep.tile([NQ, 2, PACK, P], F32, name="probs")
+        sums = keep.tile([NQ, 6], F32, name="sums")
+        turned = [psum1.tile([P, PACK, NQ], F32, name=f"side{h}") for h in range(2)]
+
+        def exponentials(h, u, floor):
+            blocks = slice(2 * u, 2 * u + 2)
+            nc.scalar.activation(
+                probs[:, h, blocks],
+                banks[0][:, blocks] if h == 0 else banks[1 + u][:],
+                ACT.Exp,
+                bias=floor,
+                scale=-1.0,
+                accum_out=sums[:, 2 * h + u : 2 * h + u + 1],
+            )
+            for j in range(PACK)[blocks]:
+                nc.tensor.transpose(turned[h][:, j, :], probs[:, h, j, :], ident[:])
+
+        for u in range(2):
+            nc.vector.tensor_scalar(
+                spare[:, 1, 2 * u : 2 * u + 2], banks[1 + u][:], 1.0, None, ALU.mult, ALU.min, accum_out=floors[:, u : u + 1]
+            )
+            exponentials(1, u, floors[:, u : u + 1])
+        nc.vector.tensor_scalar(
+            spare[:, 0], banks[0][:], floors[:, 0:1], floors[:, 1:2], ALU.min, ALU.min, accum_out=floors[:, 2:3]
+        )
+        factors = keep.tile([NQ, 2], F32, name="factors")
+        nc.scalar.activation(factors[:], floors[:, 0:2], ACT.Exp, bias=floors[:, 2:3], scale=-1.0)
+        spread = psum1.tile([P, 2, NQ], F32, name="raw1")
+        for u in range(2):
+            nc.tensor.transpose(spread[:, u, :], factors[:, u : u + 1].to_broadcast([NQ, P]), ident[:])
+        for u in range(2):
+            exponentials(0, u, floors[:, 2:3])
+
+        early = keep.tile([P, NQ, PACK], F32, name="early")
+        nc.vector.tensor_tensor(
+            early[:],
+            turned[1][:].rearrange("s j q -> s q j"),
+            ts_cols[:, 1, :].unsqueeze(1).to_broadcast([P, NQ, PACK]),
+            ALU.mult,
+        )
         w_codes = keep.tile([P, 2, NQ], U32, name="w_codes", align_bytes=64)
         w_scales = keep.tile([P, 2, NQ], U8, name="w_scales", align_bytes=64)
         w = [keep.tile([P, NQ, PACK], BF16, name=f"w{h}", align_bytes=64) for h in range(2)]
-        turned = [psum1.tile([P, PACK, NQ], F32, name=f"side{h}") for h in range(2)]
-        for h in range(2):
-            for j in range(PACK):
-                nc.tensor.transpose(turned[h][:, j, :], probs[:, h, j, :], ident[:])
+        nc.vector.tensor_tensor(
+            w[1][:].rearrange("s q (u e) -> s q u e", u=2),
+            spread[:].rearrange("s u q -> s q u").unsqueeze(3).to_broadcast([P, NQ, 2, 2]),
+            early[:].rearrange("s q (u e) -> s q u e", u=2),
+            ALU.mult,
+        )
+
+        for u in range(2):
+            nc.scalar.activation(sums[:, 4 + u : 5 + u], sums[:, 2 + u : 3 + u], ACT.Copy, scale=factors[:, u : u + 1])
+        terms_copy = keep.tile([NQ, 2, 2], F32, name="terms_copy")
+        total = keep.tile([NQ, 1], F32, name="total")
+        nc.scalar.activation(terms_copy[:], sums[:].rearrange("q (a u) -> q a u", u=2)[:, ::2], ACT.Copy, accum_out=total[:])
 
         def weigh(h, part):
             nc.vector.tensor_tensor(
@@ -261,32 +284,43 @@ def tile_attend_x_mla_alibi_srt_kernel(tc, qT, cT, ts, pos, slope, ch, offs, out
             )
 
         parts = (slice(0, NQ // 2), slice(NQ // 2, NQ))
-        weigh(0, slice(0, NQ))
-        weigh(1, parts[0])
-        quantise_weights(0, slice(0, NQ))
-        weigh(1, parts[1])
+        weigh(0, parts[0])
+        quantise_weights(1, slice(0, NQ))
+        weigh(0, parts[1])
         for part in parts:
-            quantise_weights(1, part)
+            quantise_weights(0, part)
+
+        val_codes = keep.tile([P, 2 * D], U32, name="latents0", align_bytes=64)
+        val_scales = keep.tile([P, 2 * D], U8, name="val_scales", align_bytes=64)
+        val_words = values[:].rearrange("s h v t c u -> s (h v t c u)")
+        step = 2 * D // 4
+        for first in range(0, 2 * D, step):
+            nc.vector.quantize_mx(
+                out=val_codes[:, first : first + step].bitcast(FP8X4),
+                scales=val_scales[:, first : first + step],
+                in_=val_words[:, 2 * first : 2 * (first + step)].bitcast(BF16),
+            )
         inverse = keep.tile([NQ, 1], F32, name="inverse")
         nc.vector.reciprocal(inverse[:], total[:])
 
-        outputs = [psum1.tile([NQ, D // 2], F32, name=f"raw{v}") for v in range(2)]
-        for h in range(2):
-            for v in range(2):
-                cols = slice(D // 2 * v, D // 2 * (v + 1))
+        width = D // PIECES
+        outputs = [psum1.tile([NQ, width], F32, name=name) for name in ("raw0", "scores1", "scores2", "raw1")]
+        for h in (1, 0):
+            for v in range(PIECES):
+                cols = slice(D * h + width * v, D * h + width * (v + 1))
                 nc.tensor.matmul_mx(
                     out=outputs[v][:],
                     lhsT=w_codes[:, h, :].bitcast(FP8X4),
                     lhsT_scale=w_scales[:, h, :],
-                    rhs=val_codes[:, h, cols].bitcast(FP8X4),
-                    rhs_scale=val_scales[:, h, cols],
-                    start=(h == 0),
-                    stop=(h == 1),
+                    rhs=val_codes[:, cols].bitcast(FP8X4),
+                    rhs_scale=val_scales[:, cols],
+                    start=(h == 1),
+                    stop=(h == 0),
                 )
         result = keep.tile([NQ, P, PACK], F32, name="result")
         ch_view = ch_sb[:].rearrange("q (e t) -> q e t", t=PACK)
-        for v, queue in enumerate((nc.scalar, nc.sync)):
-            part = slice(P // 2 * v, P // 2 * (v + 1))
+        for v in range(PIECES):
+            part = slice(P // PIECES * v, P // PIECES * (v + 1))
             nc.vector.scalar_tensor_tensor(
                 result[:, part],
                 outputs[v][:].rearrange("q (t e) -> q e t", t=PACK),
@@ -295,6 +329,9 @@ def tile_attend_x_mla_alibi_srt_kernel(tc, qT, cT, ts, pos, slope, ch, offs, out
                 ALU.mult,
                 ALU.mult,
             )
-            queue.dma_start(
-                out=out[0][:, D // 2 * v : D // 2 * (v + 1)], in_=result[:, part].rearrange("q e t -> q (e t)")
-            )
+            if v % 2 == 1:
+                queue = nc.scalar if v == 1 else nc.sync
+                queue.dma_start(
+                    out=out[0][:, width * (v - 1) : width * (v + 1)],
+                    in_=result[:, P // PIECES * (v - 1) : part.stop].rearrange("q e t -> q (e t)"),
+                )

@@ -142,8 +142,8 @@ def tile_attend_x_mla_alibi_srt_kernel(tc, qT, cT, ts, pos, slope, ch, offs, out
         gather_whole(0)
         turn_values(0)
         ts_cols = columns(pick(tsw, "ts"), TS_ROWS, "ts", "raw")
-        minus_ts = keep.tile([P, 2, PACK], F32, name="minus_ts")
-        nc.scalar.activation(minus_ts[:], ts_cols[:], ACT.Copy, scale=-1.0)
+        minus_ts = values[:, 1, ::2, 3, :2]
+        nc.scalar.activation(minus_ts, ts_cols[:].rearrange("s h (u e) -> s e h u", u=2), ACT.Copy, scale=-1.0)
         gather_whole(1)
         turn_values(1)
         interleave(nc.scalar.copy, 0, 0)
@@ -172,7 +172,6 @@ def tile_attend_x_mla_alibi_srt_kernel(tc, qT, cT, ts, pos, slope, ch, offs, out
         for j in range(PACK):
             nc.tensor.transpose(late[:, j, :], late_words[:, 2 * P * j + 1 : 2 * P * (j + 1) : 2], ident[:])
         late_values = late[:].bitcast(BF16).rearrange("s j (v c t) -> s v t c j", v=PIECES, t=2)
-        nc.scalar.copy(values[:, 1, :, 3].bitcast(BF16), late_values[:, :, 1])
 
         def scores(h, blocks, bank_name):
             cols = slice(P * blocks[0], P * (blocks[-1] + 1))
@@ -203,8 +202,10 @@ def tile_attend_x_mla_alibi_srt_kernel(tc, qT, cT, ts, pos, slope, ch, offs, out
         for h in (1, 0):
             for j in range(PACK):
                 nc.scalar.activation(
-                    scaled[h][:, j, :], raws[h, j // 2][:, j % 2, :], ACT.Copy, scale=minus_ts[:, h, j : j + 1]
+                    scaled[h][:, j, :], raws[h, j // 2][:, j % 2, :], ACT.Copy, scale=minus_ts[:, j % 2, h, j // 2 : j // 2 + 1]
                 )
+        for part in (slice(0, 2), slice(2, 4)):
+            nc.scalar.copy(values[:, 1, part, 3].bitcast(BF16), late_values[:, part, 1])
         for h in (1, 0):
             for j in range(PACK):
                 last = j == 3 or (h == 1 and j == 1)

@@ -330,9 +330,10 @@ def tile_attend_x_mla_alibi_srt_kernel(tc, qT, cT, ts, pos, slope, ch, offs, out
                 ALU.mult,
                 ALU.mult,
             )
-            if v % 2 == 1:
-                queue = nc.scalar if v == 1 else nc.sync
+            if v > 0:
+                first = 0 if v == 1 else v
+                queue = nc.sync if v == PIECES - 1 else nc.scalar
                 queue.dma_start(
-                    out=out[0][:, width * (v - 1) : width * (v + 1)],
-                    in_=result[:, P // PIECES * (v - 1) : part.stop].rearrange("q e t -> q (e t)"),
+                    out=out[0][:, width * first : width * (v + 1)],
+                    in_=result[:, P // PIECES * first : part.stop].rearrange("q e t -> q (e t)"),
                 )

from contextlib import ExitStack

import concourse.mybir as mybir
from concourse.masks import make_identity

NQ, N, T, D = 128, 1024, 4096, 512
P = 128
PACK = 4
HALF = 512
PREFIX = T - HALF
PIECES = 4

F32 = mybir.dt.float32
BF16 = mybir.dt.bfloat16
U32 = mybir.dt.uint32
U16 = mybir.dt.uint16
U8 = mybir.dt.uint8
FP8X4 = mybir.dt.float8_e4m3fn_x4
ACT = mybir.ActivationFunctionType
ALU = mybir.AluOpType

FLOPS = 2 * 2 * NQ * N * D
BYTES = 4 * (D * T + D * NQ + 2 * T + NQ + D + NQ * D) + 2 * P * N // 16

POS_ROWS = slice(0, P, P - 1)
TS_ROWS = slice(16, P, 64)


def tile_attend_x_mla_alibi_srt_kernel(tc, qT, cT, ts, pos, slope, ch, offs, out):
    nc = tc.nc
    with ExitStack() as ctx:
        keep = ctx.enter_context(tc.tile_pool(name="keep", bufs=1))
        shared = ctx.enter_context(tc.tile_pool(name="shared", bufs=1))
        psum2 = ctx.enter_context(tc.psum_pool(name="psum2", bufs=1))
        psum1 = ctx.enter_context(tc.psum_pool(name="psum1", bufs=1))

        offsets = keep.tile([P, N // 16], U16, name="offsets")
        nc.sync.dma_start(offsets[:], offs)

        planes = {t: keep.tile([P, T], F32, name=f"plane{t}") for t in (0, 1)}
        tsw = keep.tile([P, T], F32, name="tsw")
        posw = shared.tile([P, T], F32, name="posw", offset=12 * 1024)
        slope_col = keep.tile([NQ, 1], F32, name="slope_col")
        slope_row = keep.tile([P, NQ], F32, name="slope_row")

        c_view = cT.rearrange("(p t) n -> t p n", t=PACK)
        nc.sync.dma_start(out=planes[0][:], in_=c_view[0])
        nc.sync.dma_start(out=slope_col[:], in_=slope[0])
        nc.sync.dma_start(out=planes[1][:], in_=c_view[1])
        for window, source, rows in ((posw, pos, POS_ROWS), (tsw, ts, TS_ROWS)):
            for piece, row in enumerate(range(P)[rows]):
                tokens = slice(T // 2 * piece, T // 2 * (piece + 1))
                nc.vector.memset(window[: row if row == P - 1 else P, tokens], 0.0)
                nc.scalar.dma_start(out=window[row : row + 1, tokens], in_=source[0:1, tokens])

        def pick(window, label):
            picked = keep.tile([P, N], F32, name=f"{label}_picked")
            nc.vector.tensor_copy(picked[:], window[:].indirect(offsets[:]))
            return picked

        pos_picked = pick(posw, "pos")
        planes[3] = shared.tile([P, T], F32, name="plane3", offset=0)
        q_raw = shared.tile([P, PACK, NQ], F32, name="q_raw", offset=16 * 1024)
        ch_sb = shared.tile([P, D], F32, name="ch_sb", offset=18 * 1024)
        planes[2] = shared.tile([P, T], F32, name="plane2", offset=24 * 1024)
        nc.sync.dma_start(out=planes[2][:], in_=c_view[2])
        nc.sync.dma_start(out=planes[3][:, :PREFIX], in_=c_view[3][:, :PREFIX])
        nc.sync.dma_start(out=q_raw[:], in_=qT[0].rearrange("(p t) q -> p t q", t=PACK))
        nc.sync.dma_start(out=planes[3][:, PREFIX:], in_=c_view[3][:, PREFIX:])
        nc.sync.dma_start(out=ch_sb[:], in_=ch)

        ident = keep.tile([P, P], F32, name="ident")
        make_identity(nc, ident[:])

        def columns(picked, rows, label, bank_name):
            cols = keep.tile([P, 2, PACK], F32, name=f"{label}_cols")
            both = keep.tile([P, 2, PACK, 2], F32, name=f"{label}_both")
            for h in range(2):
                turned = psum1.tile([P, PACK, P], F32, name=f"{bank_name}{h}")
                for j in range(PACK):
                    nc.tensor.transpose(turned[:, j, :], picked[:, HALF * h + j : HALF * (h + 1) : PACK], ident[:])
                for j in range(PACK):
                    nc.scalar.activation(both[:, h, j], turned[:, j, rows], ACT.Copy, accum_out=cols[:, h, j : j + 1])
            return cols

        slope_turned = psum1.tile([P, PACK, NQ], F32, name="side0")
        nc.tensor.transpose(slope_turned[:, 0, :], slope_col[:].to_broadcast([NQ, P]), ident[:])
        nc.scalar.activation(slope_row[:], slope_turned[:, 0, :], ACT.Copy, scale=-1.0)

        low = shared.tile([P, 2, 2, 2, P, 2], BF16, name="low", offset=20 * 1024)
        high = keep.tile([P, 2, 2, 2, P, 2], BF16, name="high")
        latents = [keep.tile([P, 2, 2, P, PACK], BF16, name=f"latents{h}", align_bytes=64) for h in range(2)]
        values = keep.tile([P, 2, PIECES, PACK, P // PIECES, 2], F32, name="values", align_bytes=64)

        def picked_pair(t, h):
            return (low if t < 2 else high)[:, :, :, h]

        def gather_whole(t):
            picked = low if t < 2 else high
            nc.vector.tensor_copy(
                picked[:, t % 2].rearrange("p u h s e -> p (h s) u e"), planes[t][:].indirect(offsets[:])
            )

        def gather_high(t, h):
            if h == 0:
                nc.vector.tensor_copy(
                    high[:, t - 2, :, 0].rearrange("p u s e -> p s u e"), planes[t][:, :PREFIX].indirect(offsets[:, :32])
                )
            else:
                nc.vector.tensor_copy(
                    latents[1][:, :, :, :, t].rearrange("p u e s -> p s u e"), planes[t][:].indirect(offsets[:, 32:])
                )

        def turn_values(t):
            halves = 2 if t < 3 else 1
            turned = psum2.tile([P, 2, 2, P], F32, name="turn") if t < 3 else psum1.tile([P, 1, 2, P], F32, name="raw0")
            for h in range(halves):
                for u in range(2):
                    words = picked_pair(t, h)[:, t % 2, u].rearrange("p s e -> p (s e)").bitcast(F32)
                    nc.tensor.transpose(turned[:, h, u, :], words, ident[:])
            nc.scalar.copy(values[:, :halves, :, t], turned[:].rearrange("s h u (v c) -> s h v c u", v=PIECES))

        def interleave(copy, first, h):
            copy(latents[h][:, :, :, :, first : first + 2], picked_pair(first, h).rearrange("p t u s e -> p u e s t"))

        pos_cols = columns(pos_picked, POS_ROWS, "pos", "side")
        bias = keep.tile([P, 2, PACK, NQ], F32, name="bias")
        banks = [
            psum1.tile([NQ, PACK, P], F32, name="scores0"),
            psum1.tile([NQ, 2, P], F32, name="scores1"),
            psum1.tile([NQ, 2, P], F32, name="scores2"),
        ]

        def score_block(h, j):
            return banks[0][:, j, :] if h == 0 else banks[1 + j // 2][:, j % 2, :]

        for h in range(2):
            for j in range(PACK):
                nc.scalar.activation(bias[:, h, j, :], slope_row[:], ACT.Copy, scale=pos_cols[:, h, j : j + 1])
                first = j == 0 or (h == 1 and j == 2)
                nc.tensor.matmul(score_block(h, j), bias[:, h, j, :], ident[:], start=first, stop=False, is_transpose=True)
        gather_whole(0)
        turn_values(0)
        ts_cols = columns(pick(tsw, "ts"), TS_ROWS, "ts", "raw")
        minus_ts = values[:, 1, ::2, 3, :2]
        nc.scalar.activation(minus_ts, ts_cols[:].rearrange("s h (u e) -> s e h u", u=2), ACT.Copy, scale=-1.0)
        gather_whole(1)
        turn_values(1)
        interleave(nc.scalar.copy, 0, 0)
        interleave(nc.vector.tensor_copy, 0, 1)
        gather_whole(2)
        nc.vector.tensor_copy(latents[1][:, :, :, :, 2], high[:, 0, :, 1].rearrange("p u s e -> p u e s"))
        turn_values(2)

        key_codes = [keep.tile([P, HALF], U32, name=f"key_codes{h}", align_bytes=64) for h in range(2)]
        key_scales = [keep.tile([P, HALF], U8, name=f"key_scales{h}", align_bytes=64) for h in range(2)]
        q_grouped = keep.tile([P, NQ, PACK], BF16, name="q_grouped", align_bytes=64)
        q_codes = keep.tile([P, NQ], U32, name="q_codes", align_bytes=64)
        q_scales = keep.tile([P, NQ], U8, name="q_scales", align_bytes=64)

        for h in range(2):
            gather_high(3, h)
        nc.gpsimd.tensor_copy(q_grouped[:], q_raw[:].rearrange("p t q -> p q t"))
        interleave(nc.scalar.copy, 2, 0)
        nc.vector.quantize_mx(
            out=q_codes[:].bitcast(FP8X4), scales=q_scales[:], in_=q_grouped[:].rearrange("p q t -> p (q t)")
        )
        turn_values(3)

        late = psum2.tile([P, PACK, P], F32, name="turn")
        late_words = latents[1][:].rearrange("p u e s t -> p (u e s t)").bitcast(F32)
        for j in range(PACK):
            nc.tensor.transpose(late[:, j, :], late_words[:, 2 * P * j + 1 : 2 * P * (j + 1) : 2], ident[:])
        late_values = late[:].bitcast(BF16).rearrange("s j (v c t) -> s v t c j", v=PIECES, t=2)

        def scores(h, blocks, bank_name):
            cols = slice(P * blocks[0], P * (blocks[-1] + 1))
            nc.vector.quantize_mx(
                out=key_codes[h][:, cols].bitcast(FP8X4),
                scales=key_scales[h][:, cols],
                in_=latents[h][:].rearrange("p u e s t -> p (u e s t)")[:, PACK * cols.start : PACK * cols.stop],
            )
            raw = psum1.tile([P, len(blocks), NQ], F32, name=bank_name)
            for i, j in enumerate(blocks):
                block = slice(P * j, P * (j + 1))
                nc.tensor.matmul_mx(
                    out=raw[:, i, :],
                    lhsT=key_codes[h][:, block].bitcast(FP8X4),
                    lhsT_scale=key_scales[h][:, block],
                    rhs=q_codes[:].bitcast(FP8X4),
                    rhs_scale=q_scales[:],
                    start=True,
                    stop=True,
                )
            return raw

        raws = {
            (h, u): scores(h, range(2 * u, 2 * u + 2), name)
            for (h, u), name in zip(((1, 0), (1, 1), (0, 0), (0, 1)), ("side0", "raw1", "side1", "raw0"))
        }
        scaled = [keep.tile([P, PACK, NQ], F32, name=f"scaled{h}") for h in range(2)]
        for h in (1, 0):
            for j in range(PACK):
                nc.scalar.activation(
                    scaled[h][:, j, :], raws[h, j // 2][:, j % 2, :], ACT.Copy, scale=minus_ts[:, j % 2, h, j // 2 : j // 2 + 1]
                )
        for part in (slice(0, 2), slice(2, 4)):
            nc.scalar.copy(values[:, 1, part, 3].bitcast(BF16), late_values[:, part, 1])
        for h in (1, 0):
            for j in range(PACK):
                last = j == 3 or (h == 1 and j == 1)
                nc.tensor.matmul(score_block(h, j), scaled[h][:, j, :], ident[:], start=False, stop=last, is_transpose=True)

        spare = keep.tile([NQ, 2, PACK, P], F32, name="spare")
        floors = keep.tile([NQ, 3], F32, name="floors")
        probs = keep.tile([NQ, 2, PACK, P], F32, name="probs")
        sums = keep.tile([NQ, 6], F32, name="sums")
        turned = [psum1.tile([P, PACK, NQ], F32, name=f"side{h}") for h in range(2)]

        def exponentials(h, u, floor):
            blocks = slice(2 * u, 2 * u + 2)
            nc.scalar.activation(
                probs[:, h, blocks],
                banks[0][:, blocks] if h == 0 else banks[1 + u][:],
                ACT.Exp,
                bias=floor,
                scale=-1.0,
                accum_out=sums[:, 2 * h + u : 2 * h + u + 1],
            )
            for j in range(PACK)[blocks]:
                nc.tensor.transpose(turned[h][:, j, :], probs[:, h, j, :], ident[:])

        for u in range(2):
            nc.vector.tensor_scalar(
                spare[:, 1, 2 * u : 2 * u + 2], banks[1 + u][:], 1.0, None, ALU.mult, ALU.min, accum_out=floors[:, u : u + 1]
            )
            exponentials(1, u, floors[:, u : u + 1])
        nc.vector.tensor_scalar(
            spare[:, 0], banks[0][:], floors[:, 0:1], floors[:, 1:2], ALU.min, ALU.min, accum_out=floors[:, 2:3]
        )
        factors = keep.tile([NQ, 2], F32, name="factors")
        nc.scalar.activation(factors[:], floors[:, 0:2], ACT.Exp, bias=floors[:, 2:3], scale=-1.0)
        spread = psum1.tile([P, 2, NQ], F32, name="raw1")
        for u in range(2):
            nc.tensor.transpose(spread[:, u, :], factors[:, u : u + 1].to_broadcast([NQ, P]), ident[:])
        for u in range(2):
            exponentials(0, u, floors[:, 2:3])

        early = keep.tile([P, NQ, PACK], F32, name="early")
        nc.vector.tensor_tensor(
            early[:],
            turned[1][:].rearrange("s j q -> s q j"),
            ts_cols[:, 1, :].unsqueeze(1).to_broadcast([P, NQ, PACK]),
            ALU.mult,
        )
        w_codes = keep.tile([P, 2, NQ], U32, name="w_codes", align_bytes=64)
        w_scales = keep.tile([P, 2, NQ], U8, name="w_scales", align_bytes=64)
        w = [keep.tile([P, NQ, PACK], BF16, name=f"w{h}", align_bytes=64) for h in range(2)]
        nc.vector.tensor_tensor(
            w[1][:].rearrange("s q (u e) -> s q u e", u=2),
            spread[:].rearrange("s u q -> s q u").unsqueeze(3).to_broadcast([P, NQ, 2, 2]),
            early[:].rearrange("s q (u e) -> s q u e", u=2),
            ALU.mult,
        )

        for u in range(2):
            nc.scalar.activation(sums[:, 4 + u : 5 + u], sums[:, 2 + u : 3 + u], ACT.Copy, scale=factors[:, u : u + 1])
        terms_copy = keep.tile([NQ, 2, 2], F32, name="terms_copy")
        total = keep.tile([NQ, 1], F32, name="total")
        nc.scalar.activation(terms_copy[:], sums[:].rearrange("q (a u) -> q a u", u=2)[:, ::2], ACT.Copy, accum_out=total[:])

        def weigh(h, part):
            nc.vector.tensor_tensor(
                w[h][:, part],
                turned[h][:, :, part].rearrange("s j q -> s q j"),
                ts_cols[:, h, :].unsqueeze(1).to_broadcast([P, part.stop - part.start, PACK]),
                ALU.mult,
            )

        def quantise_weights(h, part):
            nc.vector.quantize_mx(
                out=w_codes[:, h, part].bitcast(FP8X4),
                scales=w_scales[:, h, part],
                in_=w[h][:, part].rearrange("s q j -> s (q j)"),
            )

        parts = (slice(0, NQ // 2), slice(NQ // 2, NQ))
        weigh(0, parts[0])
        quantise_weights(1, slice(0, NQ))
        weigh(0, parts[1])
        for part in parts:
            quantise_weights(0, part)

        val_codes = keep.tile([P, 2 * D], U32, name="latents0", align_bytes=64)
        val_scales = keep.tile([P, 2 * D], U8, name="val_scales", align_bytes=64)
        val_words = values[:].rearrange("s h v t c u -> s (h v t c u)")
        step = 2 * D // 4
        for first in range(0, 2 * D, step):
            nc.vector.quantize_mx(
                out=val_codes[:, first : first + step].bitcast(FP8X4),
                scales=val_scales[:, first : first + step],
                in_=val_words[:, 2 * first : 2 * (first + step)].bitcast(BF16),
            )
        inverse = keep.tile([NQ, 1], F32, name="inverse")
        nc.vector.reciprocal(inverse[:], total[:])

        width = D // PIECES
        outputs = [psum1.tile([NQ, width], F32, name=name) for name in ("raw0", "scores1", "scores2", "raw1")]
        for h in (1, 0):
            for v in range(PIECES):
                cols = slice(D * h + width * v, D * h + width * (v + 1))
                nc.tensor.matmul_mx(
                    out=outputs[v][:],
                    lhsT=w_codes[:, h, :].bitcast(FP8X4),
                    lhsT_scale=w_scales[:, h, :],
                    rhs=val_codes[:, cols].bitcast(FP8X4),
                    rhs_scale=val_scales[:, cols],
                    start=(h == 1),
                    stop=(h == 0),
                )
        result = keep.tile([NQ, P, PACK], F32, name="result")
        ch_view = ch_sb[:].rearrange("q (e t) -> q e t", t=PACK)
        for v in range(PIECES):
            part = slice(P // PIECES * v, P // PIECES * (v + 1))
            nc.vector.scalar_tensor_tensor(
                result[:, part],
                outputs[v][:].rearrange("q (t e) -> q e t", t=PACK),
                inverse[:],
                ch_view[:, part],
                ALU.mult,
                ALU.mult,
            )
            if v > 0:
                first = 0 if v == 1 else v
                queue = nc.sync if v == PIECES - 1 else nc.scalar
                queue.dma_start(
                    out=out[0][:, width * first : width * (v + 1)],
                    in_=result[:, P // PIECES * first : part.stop].rearrange("q e t -> q (e t)"),
                )
